import numpy as np
import ml_dtypes


def mxq(x, axis, fmt="e4m3"):
    dtype, down = {"e4m3": (ml_dtypes.float8_e4m3fn, 7), "e5m2": (ml_dtypes.float8_e5m2, 14)}[fmt]
    v = np.moveaxis(np.asarray(x, np.float32).astype(ml_dtypes.bfloat16).astype(np.float64), axis, -1)
    blocks = v.reshape(v.shape[:-1] + (-1, 32))
    amax = np.abs(blocks).max(-1, keepdims=True)
    byte = np.maximum(np.where(amax > 0, np.frexp(amax)[1] - 1 + 127, 0) - down, 1)
    scale = np.exp2(byte - 127.0)
    codes = (blocks / scale).astype(np.float32).astype(dtype).astype(np.float64)
    return np.moveaxis((codes * scale).reshape(v.shape), -1, axis)


WIDE = False


def mx_kscale(k):
    if not WIDE:
        return np.ones(k)
    levels = np.array([10, -10, 5, -5, 0])
    if k % 512:
        return np.exp2(np.random.permutation(np.resize(levels, k // 32))).repeat(32)
    a = np.empty((k // 512, 16))
    for p in range(k // 512):
        a[p, :8] = np.random.permutation(np.resize(levels, 8))
        for g in range(8):
            far = levels[np.abs(levels - a[p, g]) >= 10]
            a[p, g + 8] = far[np.random.randint(len(far))]
    return np.exp2(a.ravel()).repeat(32)


def f64(x):
    return np.asarray(x).astype(np.float64)


E2M1 = np.array([0.0, 0.5, 1.0, 1.5, 2.0, 3.0, 4.0, 6.0, -0.0, -0.5, -1.0, -1.5, -2.0, -3.0, -4.0, -6.0])


def pack_weight(w, fmt):
    k, n = w.shape
    w = f64(np.asarray(w, np.float32).astype(ml_dtypes.bfloat16)).reshape(k // 32, 32, n)
    amax = np.abs(w).max(1)
    if fmt == "e4m3":
        byte = np.frexp(amax)[1] - 1 + 127 - 7
    else:
        mant, ex = np.frexp(amax / 6.0)
        byte = np.where(mant > 0.5, ex, ex - 1) + 127
    byte = np.clip(np.where(amax > 0, byte, 1), 1, 254)
    scaled = (w * np.exp2(127.0 - byte)[:, None, :]).reshape(k, n).astype(np.float32)
    by_word = np.ascontiguousarray(scaled.reshape(k // 512, 128, 4, n).transpose(0, 1, 3, 2))
    if fmt == "e4m3":
        words = by_word.astype(ml_dtypes.float8_e4m3fn).view(np.uint8)
    else:
        c = by_word.astype(ml_dtypes.float4_e2m1fn).view(np.uint8) & 0xF
        words = (c[..., 0::2] | (c[..., 1::2] << 4)).reshape(k // 512, 128, 2 * n)
    return np.ascontiguousarray(words), np.ascontiguousarray(byte.astype(np.uint8).reshape(k // 512, 16, n))


def unpack_weight(words, scales, fmt):
    g, _, n = scales.shape
    words = np.ascontiguousarray(words).reshape(g, 128, n, -1)
    if fmt == "e4m3":
        vals = words.view(ml_dtypes.float8_e4m3fn).astype(np.float64)
    else:
        nib = np.empty((g, 128, n, 4), np.uint8)
        nib[..., 0::2] = words & 0xF
        nib[..., 1::2] = words >> 4
        vals = E2M1[nib]
    vals = vals * np.repeat(np.exp2(scales.astype(np.float64) - 127.0), 8, axis=1)[..., None]
    return vals.transpose(0, 1, 3, 2).reshape(g * 512, n)


def gelu(v):
    return 0.5 * v * (1.0 + np.tanh(np.sqrt(2.0 / np.pi) * (v + 0.044715 * v**3)))


K, M, T = 512, 512, 1536


def setup_inputs():
    n = np.random.standard_normal
    s = mx_kscale(K)[:, None]
    w = n((K, M)) / np.sqrt(K) / s
    w4 = pack_weight(w, "e2m1")
    rest = w - unpack_weight(*w4, "e2m1")
    p_r8 = pack_weight(rest, "e4m3")
    return {
        "x": (n((K, T)) * s).astype(np.float32),
        "w4_words": w4[0],
        "w4_scales": w4[1],
        "r8_words": p_r8[0],
        "r8_scales": p_r8[1],
        "b": (0.3 * n(512)).astype(np.float32),
    }


def reference(x, w4_words, w4_scales, r8_words, r8_scales, b):
    x_ = mxq(f64(x), 0, "e4m3")
    w4_ = unpack_weight(w4_words, w4_scales, "e2m1")
    r8_ = unpack_weight(r8_words, r8_scales, "e4m3")
    y = x_.T @ w4_ + x_.T @ r8_
    return gelu(y + f64(b)[None, :])

@@ -1,0 +1,141 @@
+from contextlib import ExitStack
+
+import concourse.mybir as mybir
+from concourse.masks import make_identity
+
+K, N, T = 512, 512, 1536
+FLOPS = 2 * 2 * K * N * T
+
+F32 = mybir.dt.float32
+BF16 = mybir.dt.bfloat16
+I32 = mybir.dt.int32
+U32 = mybir.dt.uint32
+U8 = mybir.dt.uint8
+FP8X4 = mybir.dt.float8_e4m3fn_x4
+FP4X4 = mybir.dt.float4_e2m1fn_x4
+GELU = mybir.ActivationFunctionType.Gelu_apprx_tanh
+MULT = mybir.AluOpType.mult
+ADD = mybir.AluOpType.add
+
+P = 128
+TILES = T // P
+CHUNKS = [128,256,256,256,256,256,128]
+COPY_ENGINE = ["V","V","G","S","G","S","V","S","S","V","VS","G"]
+
+
+def tile_mix_resid_tm_gelu_kernel(tc, x, w4_words, w4_scales, r8_words, r8_scales, b, out):
+    nc = tc.nc
+    with ExitStack() as ctx:
+        keep = ctx.enter_context(tc.tile_pool(name="keep", bufs=1))
+        psum = ctx.enter_context(tc.psum_pool(name="psum", bufs=7))
+        psum_b = ctx.enter_context(tc.psum_pool(name="psum_b", bufs=1))
+        ctx.enter_context(tc.manual_schedule())
+
+        w4_plane = keep.tile([P, N], U8, align_bytes=64, name="w4_plane")
+        r8_plane = keep.tile([P, N], U8, align_bytes=64, name="r8_plane")
+        w4 = keep.tile([P, 2 * N], U8, align_bytes=64, name="w4")
+        r8 = keep.tile([P, 4 * N], U8, align_bytes=64, name="r8")
+        warm = keep.tile([P, 1], F32, name="warm")
+        b_cols = keep.tile([P, 4], F32, name="b_cols")
+        bias = keep.tile([P, N], F32, name="bias")
+        ident = keep.tile([P, P], F32, name="ident")
+
+        xv = x.rearrange("(p j) t -> p j t", j=4)
+        raws = []
+        starts = []
+        t0 = 0
+        for i, w in enumerate(CHUNKS):
+            raw = keep.tile([P, 4, w], F32, name=f"raw{i}")
+            raws.append(raw)
+            starts.append(t0)
+            t0 += w
+
+        def load_x(i):
+            nc.sync.dma_start(out=raws[i][:], in_=xv[:, :, starts[i] : starts[i] + CHUNKS[i]])
+
+        nc.vector.memset(w4_plane[:].bitcast(I32), 0)
+        nc.vector.memset(r8_plane[:].bitcast(I32), 0)
+        nc.vector.memset(ident[:], 0.0)
+        nc.vector.memset(warm[:], 0.0)
+        nc.scalar.activation(out=warm[:], in_=warm[:], func=GELU)
+
+        def load_scales(plane, scales):
+            for q in range(4):
+                nc.sync.dma_start(out=plane[32 * q : 32 * q + 4, :].bitcast(I32), in_=scales[0, 4 * q : 4 * q + 4, :].bitcast(I32))
+
+        nc.sync.dma_start(out=b_cols[:], in_=b.rearrange("(p m) -> p m", m=4))
+        nc.gpsimd.dma_start(out=w4[:].bitcast(I32), in_=w4_words[0].bitcast(I32))
+        make_identity(nc, ident[:], nomemset=True)
+        load_x(0)
+        load_scales(w4_plane, w4_scales)
+        load_x(1)
+        nc.sync.dma_start(out=r8[:].bitcast(I32), in_=r8_words[0].rearrange("p n i -> p (n i)").bitcast(I32))
+        load_scales(r8_plane, r8_scales)
+
+        for i in range(2, len(CHUNKS)):
+            load_x(i)
+
+        b_ps = psum_b.tile([P, 4, P], F32, name="b_ps")
+        for m in range(4):
+            nc.tensor.transpose(b_ps[:, m, :], b_cols[:, m : m + 1].to_broadcast([P, P]), ident[:])
+
+        grouped = {}
+        codes = {}
+        planes = {}
+        accs = {}
+
+        def copy(i):
+            c = max(j for j in range(len(CHUNKS)) if starts[j] <= i * P)
+            lo = i * P - starts[c]
+            g = keep.tile([P, P, 4], BF16, align_bytes=64, name=f"grouped{i}")
+            grouped[i] = g
+            w = P // len(COPY_ENGINE[i])
+            for n, e in enumerate(COPY_ENGINE[i]):
+                dst = g[:, n * w : (n + 1) * w, :].rearrange("p (c i) j -> p c j i", i=4)
+                src = raws[c][:, :, lo + n * w : lo + (n + 1) * w].rearrange("p j (c i) -> p c j i", i=4)
+                if e == "V":
+                    nc.vector.tensor_copy(out=dst, in_=src)
+                elif e == "S":
+                    nc.scalar.copy(out=dst, in_=src)
+                else:
+                    nc.gpsimd.tensor_scalar(out=dst, in0=src, scalar1=1.0, scalar2=0.0, op0=MULT, op1=ADD)
+
+        def quantize(i):
+            cd = keep.tile([P, P], U32, align_bytes=64, name=f"codes{i}")
+            pl = keep.tile([P, P], U8, align_bytes=64, name=f"plane{i}")
+            codes[i] = cd
+            planes[i] = pl
+            nc.vector.quantize_mx(out=cd[:].bitcast(FP8X4), scales=pl[:], in_=grouped[i][:].rearrange("p w j -> p (w j)"))
+
+        def multiply(i):
+            acc = psum.tile([P, N], F32, name="acc")
+            accs[i] = acc
+            nc.tensor.matmul_mx(out=acc[:], lhsT=codes[i][:].bitcast(FP8X4), lhsT_scale=planes[i][:],
+                                rhs=w4[:].bitcast(FP4X4), rhs_scale=w4_plane[:], start=True, stop=False)
+            nc.tensor.matmul_mx(out=acc[:], lhsT=codes[i][:].bitcast(FP8X4), lhsT_scale=planes[i][:],
+                                rhs=r8[:].bitcast(FP8X4), rhs_scale=r8_plane[:], start=False, stop=True)
+
+        def finish(i):
+            y = keep.tile([P, N], F32, name=f"y{i}")
+            o = keep.tile([P, N], F32, name=f"o{i}")
+            w = N // 2 if i == TILES - 1 else N
+            for n0 in range(0, N, w):
+                cols = slice(n0, n0 + w)
+                nc.vector.tensor_tensor(out=y[:, cols], in0=accs[i][:, cols], in1=bias[:, cols], op=ADD)
+                nc.scalar.activation(out=o[:, cols], in_=y[:, cols], func=GELU)
+                nc.sync.dma_start(out=out[i * P : (i + 1) * P, cols], in_=o[:, cols])
+
+        nc.scalar.copy(out=bias[:].rearrange("t (p m) -> t p m", m=4), in_=b_ps[:].rearrange("t m p -> t p m"))
+        copied = 0
+        quantized = 0
+        for i in range(TILES):
+            while copied < min(TILES, i + 4 + 1):
+                copy(copied)
+                copied += 1
+            ready = quantized
+            ahead = 2 if i < 0 else 2
+            while quantized < min(TILES, i + ahead + 1):
+                quantize(quantized)
+                multiply(quantized)
+                quantized += 1
+            finish(i)

@@ -19,20 +19,21 @@ ADD = mybir.AluOpType.add
 
 P = 128
 TILES = T // P
-CHUNKS = [128,256,256,256,256,256,128]
-COPY_ENGINE = ["V","V","G","S","G","S","V","S","S","V","VS","G"]
+CHUNKS = [128, 256, 256, 256, 256, 256, 128]
 
 
 def tile_mix_resid_tm_gelu_kernel(tc, x, w4_words, w4_scales, r8_words, r8_scales, b, out):
     nc = tc.nc
     with ExitStack() as ctx:
         keep = ctx.enter_context(tc.tile_pool(name="keep", bufs=1))
+        stage = ctx.enter_context(tc.tile_pool(name="stage", bufs=1))
         psum = ctx.enter_context(tc.psum_pool(name="psum", bufs=7))
         psum_b = ctx.enter_context(tc.psum_pool(name="psum_b", bufs=1))
         ctx.enter_context(tc.manual_schedule())
 
-        w4_plane = keep.tile([P, N], U8, align_bytes=64, name="w4_plane")
-        r8_plane = keep.tile([P, N], U8, align_bytes=64, name="r8_plane")
+        w_planes = keep.tile([P, 2 * N], U8, align_bytes=64, name="w_planes")
+        w4_plane = w_planes[:, 0:N]
+        r8_plane = w_planes[:, N : 2 * N]
         w4 = keep.tile([P, 2 * N], U8, align_bytes=64, name="w4")
         r8 = keep.tile([P, 4 * N], U8, align_bytes=64, name="r8")
         warm = keep.tile([P, 1], F32, name="warm")
@@ -41,101 +42,107 @@ def tile_mix_resid_tm_gelu_kernel(tc, x, w4_words, w4_scales, r8_words, r8_scale
         ident = keep.tile([P, P], F32, name="ident")
 
         xv = x.rearrange("(p j) t -> p j t", j=4)
-        raws = []
-        starts = []
-        t0 = 0
-        for i, w in enumerate(CHUNKS):
-            raw = keep.tile([P, 4, w], F32, name=f"raw{i}")
-            raws.append(raw)
-            starts.append(t0)
-            t0 += w
+        starts = [sum(CHUNKS[:c]) for c in range(len(CHUNKS))]
+        raws = [keep.tile([P, 4, w], F32, name=f"raw{c}") for c, w in enumerate(CHUNKS)]
 
-        def load_x(i):
-            nc.sync.dma_start(out=raws[i][:], in_=xv[:, :, starts[i] : starts[i] + CHUNKS[i]])
+        def load_x(c):
+            nc.sync.dma_start(out=raws[c][:], in_=xv[:, :, starts[c] : starts[c] + CHUNKS[c]])
 
-        nc.vector.memset(w4_plane[:].bitcast(I32), 0)
-        nc.vector.memset(r8_plane[:].bitcast(I32), 0)
+        def load_scales(queue, col, scales, q):
+            queue.dma_start(
+                out=w_planes[32 * q : 32 * q + 4, col : col + N].bitcast(I32),
+                in_=scales[0, 4 * q : 4 * q + 4, :].bitcast(I32),
+            )
+
+        nc.vector.memset(w_planes[:].bitcast(I32), 0)
         nc.vector.memset(ident[:], 0.0)
         nc.vector.memset(warm[:], 0.0)
         nc.scalar.activation(out=warm[:], in_=warm[:], func=GELU)
-
-        def load_scales(plane, scales):
-            for q in range(4):
-                nc.sync.dma_start(out=plane[32 * q : 32 * q + 4, :].bitcast(I32), in_=scales[0, 4 * q : 4 * q + 4, :].bitcast(I32))
 
         nc.sync.dma_start(out=b_cols[:], in_=b.rearrange("(p m) -> p m", m=4))
         nc.gpsimd.dma_start(out=w4[:].bitcast(I32), in_=w4_words[0].bitcast(I32))
         make_identity(nc, ident[:], nomemset=True)
         load_x(0)
-        load_scales(w4_plane, w4_scales)
+        for q in range(4):
+            load_scales(nc.sync, 0, w4_scales, q)
         load_x(1)
         nc.sync.dma_start(out=r8[:].bitcast(I32), in_=r8_words[0].rearrange("p n i -> p (n i)").bitcast(I32))
-        load_scales(r8_plane, r8_scales)
-
-        for i in range(2, len(CHUNKS)):
-            load_x(i)
+        for q in range(4):
+            load_scales(nc.sync, N, r8_scales, q)
+        for c in range(2, len(CHUNKS)):
+            load_x(c)
 
         b_ps = psum_b.tile([P, 4, P], F32, name="b_ps")
         for m in range(4):
             nc.tensor.transpose(b_ps[:, m, :], b_cols[:, m : m + 1].to_broadcast([P, P]), ident[:])
 
         grouped = {}
-        codes = {}
-        planes = {}
         accs = {}
+        sums = {}
 
-        def copy(i):
+        def copy(i, engine):
             c = max(j for j in range(len(CHUNKS)) if starts[j] <= i * P)
             lo = i * P - starts[c]
-            g = keep.tile([P, P, 4], BF16, align_bytes=64, name=f"grouped{i}")
+            if engine == "G":
+                g = stage.tile([P, P, 4], BF16, align_bytes=64, name="staged")
+            else:
+                g = keep.tile([P, P, 4], BF16, align_bytes=64, name=f"grouped{i}")
             grouped[i] = g
-            w = P // len(COPY_ENGINE[i])
-            for n, e in enumerate(COPY_ENGINE[i]):
-                dst = g[:, n * w : (n + 1) * w, :].rearrange("p (c i) j -> p c j i", i=4)
-                src = raws[c][:, :, lo + n * w : lo + (n + 1) * w].rearrange("p j (c i) -> p c j i", i=4)
-                if e == "V":
-                    nc.vector.tensor_copy(out=dst, in_=src)
-                elif e == "S":
-                    nc.scalar.copy(out=dst, in_=src)
-                else:
-                    nc.gpsimd.tensor_scalar(out=dst, in0=src, scalar1=1.0, scalar2=0.0, op0=MULT, op1=ADD)
+            dst = g[:].rearrange("p (c i) j -> p c j i", i=4)
+            src = raws[c][:, :, lo : lo + P].rearrange("p j (c i) -> p c j i", i=4)
+            if engine == "V":
+                nc.vector.tensor_copy(out=dst, in_=src)
+            elif engine == "S":
+                nc.scalar.copy(out=dst, in_=src)
+            else:
+                nc.gpsimd.tensor_scalar(out=dst, in0=src, scalar1=1.0, scalar2=0.0, op0=MULT, op1=ADD)
 
         def quantize(i):
-            cd = keep.tile([P, P], U32, align_bytes=64, name=f"codes{i}")
-            pl = keep.tile([P, P], U8, align_bytes=64, name=f"plane{i}")
-            codes[i] = cd
-            planes[i] = pl
-            nc.vector.quantize_mx(out=cd[:].bitcast(FP8X4), scales=pl[:], in_=grouped[i][:].rearrange("p w j -> p (w j)"))
-
-        def multiply(i):
+            codes = keep.tile([P, P], U32, align_bytes=64, name=f"codes{i}")
+            plane = keep.tile([P, P], U8, align_bytes=64, name=f"plane{i}")
+            nc.vector.quantize_mx(out=codes[:].bitcast(FP8X4), scales=plane[:], in_=grouped[i][:].rearrange("p w j -> p (w j)"))
             acc = psum.tile([P, N], F32, name="acc")
             accs[i] = acc
-            nc.tensor.matmul_mx(out=acc[:], lhsT=codes[i][:].bitcast(FP8X4), lhsT_scale=planes[i][:],
-                                rhs=w4[:].bitcast(FP4X4), rhs_scale=w4_plane[:], start=True, stop=False)
-            nc.tensor.matmul_mx(out=acc[:], lhsT=codes[i][:].bitcast(FP8X4), lhsT_scale=planes[i][:],
-                                rhs=r8[:].bitcast(FP8X4), rhs_scale=r8_plane[:], start=False, stop=True)
+            nc.tensor.matmul_mx(out=acc[:], lhsT=codes[:].bitcast(FP8X4), lhsT_scale=plane[:],
+                                rhs=w4[:].bitcast(FP4X4), rhs_scale=w4_plane, start=True, stop=False)
+            nc.tensor.matmul_mx(out=acc[:], lhsT=codes[:].bitcast(FP8X4), lhsT_scale=plane[:],
+                                rhs=r8[:].bitcast(FP8X4), rhs_scale=r8_plane, start=False, stop=True)
 
-        def finish(i):
-            y = keep.tile([P, N], F32, name=f"y{i}")
-            o = keep.tile([P, N], F32, name=f"o{i}")
-            w = N // 2 if i == TILES - 1 else N
-            for n0 in range(0, N, w):
-                cols = slice(n0, n0 + w)
-                nc.vector.tensor_tensor(out=y[:, cols], in0=accs[i][:, cols], in1=bias[:, cols], op=ADD)
-                nc.scalar.activation(out=o[:, cols], in_=y[:, cols], func=GELU)
-                nc.sync.dma_start(out=out[i * P : (i + 1) * P, cols], in_=o[:, cols])
+        def add(i, cols=slice(0, N)):
+            if i not in sums:
+                sums[i] = (keep.tile([P, N], F32, name=f"y{i}"), keep.tile([P, N], F32, name=f"o{i}"))
+            nc.vector.tensor_tensor(out=sums[i][0][:, cols], in0=accs[i][:, cols], in1=bias[:, cols], op=ADD)
 
+        def finish(i, cols=slice(0, N)):
+            y, o = sums[i]
+            nc.scalar.activation(out=o[:, cols], in_=y[:, cols], func=GELU)
+            nc.sync.dma_start(out=out[i * P : (i + 1) * P, cols], in_=o[:, cols])
+
+        copy(0, "V")
+        quantize(0)
         nc.scalar.copy(out=bias[:].rearrange("t (p m) -> t p m", m=4), in_=b_ps[:].rearrange("t m p -> t p m"))
-        copied = 0
-        quantized = 0
-        for i in range(TILES):
-            while copied < min(TILES, i + 4 + 1):
-                copy(copied)
-                copied += 1
-            ready = quantized
-            ahead = 2 if i < 0 else 2
-            while quantized < min(TILES, i + ahead + 1):
-                quantize(quantized)
-                multiply(quantized)
-                quantized += 1
+        copy(1, "V")
+        copy(2, "S")
+        quantize(1)
+        quantize(2)
+        copy(3, "S")
+        copy(4, "G")
+        for i in range(0, TILES - 2, 2):
+            add(i)
             finish(i)
+            if i + 5 < TILES - 1:
+                copy(i + 5, "S")
+            add(i + 1)
+            finish(i + 1)
+            if i + 5 == TILES - 1:
+                copy(TILES - 1, "V")
+            quantize(i + 3)
+            if i + 4 < TILES:
+                quantize(i + 4)
+            if i + 6 < TILES:
+                copy(i + 6, "G")
+        add(TILES - 2)
+        finish(TILES - 2)
+        for half in (slice(0, N // 2), slice(N // 2, N)):
+            add(TILES - 1, half)
+            finish(TILES - 1, half)

@@ -19,14 +19,15 @@ ADD = mybir.AluOpType.add
 
 P = 128
 TILES = T // P
-CHUNKS = [128, 256, 256, 256, 256, 256, 128]
+CHUNKS = [128, 128, 384, 256, 256, 256, 128]
+PAIR = 2 * P
+GPSIMD_SPANS = [(5 * P, 7 * P), (9 * P, 11 * P), (11 * P, 12 * P)]
 
 
 def tile_mix_resid_tm_gelu_kernel(tc, x, w4_words, w4_scales, r8_words, r8_scales, b, out):
     nc = tc.nc
     with ExitStack() as ctx:
         keep = ctx.enter_context(tc.tile_pool(name="keep", bufs=1))
-        stage = ctx.enter_context(tc.tile_pool(name="stage", bufs=1))
         psum = ctx.enter_context(tc.psum_pool(name="psum", bufs=7))
         psum_b = ctx.enter_context(tc.psum_pool(name="psum_b", bufs=1))
         ctx.enter_context(tc.manual_schedule())
@@ -40,13 +41,19 @@ def tile_mix_resid_tm_gelu_kernel(tc, x, w4_words, w4_scales, r8_words, r8_scale
         b_cols = keep.tile([P, 4], F32, name="b_cols")
         bias = keep.tile([P, N], F32, name="bias")
         ident = keep.tile([P, P], F32, name="ident")
+        grouped = keep.tile([P, 4 * T], BF16, align_bytes=64, name="grouped")
+        turn = keep.tile([P, 4 * PAIR], BF16, align_bytes=64, name="turn")
+        codes = keep.tile([P, T], U32, align_bytes=64, name="codes")
+        x_plane = keep.tile([P, T], U8, align_bytes=64, name="x_plane")
+        y = keep.tile([P, TILES * N], F32, name="y")
+        o = keep.tile([P, TILES * N], F32, name="o")
 
         xv = x.rearrange("(p j) t -> p j t", j=4)
         starts = [sum(CHUNKS[:c]) for c in range(len(CHUNKS))]
         raws = [keep.tile([P, 4, w], F32, name=f"raw{c}") for c, w in enumerate(CHUNKS)]
 
-        def load_x(c):
-            nc.sync.dma_start(out=raws[c][:], in_=xv[:, :, starts[c] : starts[c] + CHUNKS[c]])
+        def load_x(c, queue=nc.sync):
+            queue.dma_start(out=raws[c][:], in_=xv[:, :, starts[c] : starts[c] + CHUNKS[c]])
 
         def load_scales(queue, col, scales, q):
             queue.dma_start(
@@ -58,91 +65,130 @@ def tile_mix_resid_tm_gelu_kernel(tc, x, w4_words, w4_scales, r8_words, r8_scale
         nc.vector.memset(ident[:], 0.0)
         nc.vector.memset(warm[:], 0.0)
         nc.scalar.activation(out=warm[:], in_=warm[:], func=GELU)
-
-        nc.sync.dma_start(out=b_cols[:], in_=b.rearrange("(p m) -> p m", m=4))
-        nc.gpsimd.dma_start(out=w4[:].bitcast(I32), in_=w4_words[0].bitcast(I32))
         make_identity(nc, ident[:], nomemset=True)
+
         load_x(0)
         for q in range(4):
             load_scales(nc.sync, 0, w4_scales, q)
+        nc.sync.dma_start(out=w4[:].bitcast(I32), in_=w4_words[0].bitcast(I32))
         load_x(1)
+        load_x(2)
+        nc.sync.dma_start(out=b_cols[:], in_=b.rearrange("(p m) -> p m", m=4))
         nc.sync.dma_start(out=r8[:].bitcast(I32), in_=r8_words[0].rearrange("p n i -> p (n i)").bitcast(I32))
         for q in range(4):
             load_scales(nc.sync, N, r8_scales, q)
-        for c in range(2, len(CHUNKS)):
+        for c in range(3, len(CHUNKS)):
             load_x(c)
 
         b_ps = psum_b.tile([P, 4, P], F32, name="b_ps")
-        for m in range(4):
-            nc.tensor.transpose(b_ps[:, m, :], b_cols[:, m : m + 1].to_broadcast([P, P]), ident[:])
 
-        grouped = {}
+        def spread_bias():
+            for m in range(4):
+                nc.tensor.transpose(b_ps[:, m, :], b_cols[:, m : m + 1].to_broadcast([P, P]), ident[:])
+
         accs = {}
-        sums = {}
 
-        def copy(i, engine):
-            c = max(j for j in range(len(CHUNKS)) if starts[j] <= i * P)
-            lo = i * P - starts[c]
+        def staged(t0, t1):
+            if (t0, t1) in GPSIMD_SPANS:
+                return turn[:, 0 : 4 * (t1 - t0)]
+            return grouped[:, 4 * t0 : 4 * t1]
+
+        def copy(engine, t0, t1):
+            c = max(j for j in range(len(CHUNKS)) if starts[j] <= t0)
+            src = raws[c][:, :, t0 - starts[c] : t1 - starts[c]]
+            dst = staged(t0, t1)
             if engine == "G":
-                g = stage.tile([P, P, 4], BF16, align_bytes=64, name="staged")
-            else:
-                g = keep.tile([P, P, 4], BF16, align_bytes=64, name=f"grouped{i}")
-            grouped[i] = g
-            dst = g[:].rearrange("p (c i) j -> p c j i", i=4)
-            src = raws[c][:, :, lo : lo + P].rearrange("p j (c i) -> p c j i", i=4)
+                nc.gpsimd.tensor_scalar(out=dst.rearrange("p (w j) -> p w j", j=4), in0=src.rearrange("p j w -> p w j"),
+                                        scalar1=1.0, scalar2=0.0, op0=MULT, op1=ADD)
+                return
+            dst = dst.rearrange("p (c i j) -> p c j i", i=4, j=4)
+            src = src.rearrange("p j (c i) -> p c j i", i=4)
             if engine == "V":
                 nc.vector.tensor_copy(out=dst, in_=src)
-            elif engine == "S":
-                nc.scalar.copy(out=dst, in_=src)
             else:
-                nc.gpsimd.tensor_scalar(out=dst, in0=src, scalar1=1.0, scalar2=0.0, op0=MULT, op1=ADD)
+                nc.scalar.copy(out=dst, in_=src)
 
-        def quantize(i):
-            codes = keep.tile([P, P], U32, align_bytes=64, name=f"codes{i}")
-            plane = keep.tile([P, P], U8, align_bytes=64, name=f"plane{i}")
-            nc.vector.quantize_mx(out=codes[:].bitcast(FP8X4), scales=plane[:], in_=grouped[i][:].rearrange("p w j -> p (w j)"))
+        def quantize(t0, t1):
+            nc.vector.quantize_mx(out=codes[:, t0:t1].bitcast(FP8X4), scales=x_plane[:, t0:t1], in_=staged(t0, t1))
+
+        def base_pass(i):
             acc = psum.tile([P, N], F32, name="acc")
             accs[i] = acc
-            nc.tensor.matmul_mx(out=acc[:], lhsT=codes[:].bitcast(FP8X4), lhsT_scale=plane[:],
+            cols = slice(i * P, (i + 1) * P)
+            nc.tensor.matmul_mx(out=acc[:], lhsT=codes[:, cols].bitcast(FP8X4), lhsT_scale=x_plane[:, cols],
                                 rhs=w4[:].bitcast(FP4X4), rhs_scale=w4_plane, start=True, stop=False)
-            nc.tensor.matmul_mx(out=acc[:], lhsT=codes[:].bitcast(FP8X4), lhsT_scale=plane[:],
+
+        def rest_pass(i):
+            cols = slice(i * P, (i + 1) * P)
+            nc.tensor.matmul_mx(out=accs[i][:], lhsT=codes[:, cols].bitcast(FP8X4), lhsT_scale=x_plane[:, cols],
                                 rhs=r8[:].bitcast(FP8X4), rhs_scale=r8_plane, start=False, stop=True)
 
-        def add(i, cols=slice(0, N)):
-            if i not in sums:
-                sums[i] = (keep.tile([P, N], F32, name=f"y{i}"), keep.tile([P, N], F32, name=f"o{i}"))
-            nc.vector.tensor_tensor(out=sums[i][0][:, cols], in0=accs[i][:, cols], in1=bias[:, cols], op=ADD)
+        def multiply(i):
+            base_pass(i)
+            rest_pass(i)
 
-        def finish(i, cols=slice(0, N)):
-            y, o = sums[i]
-            nc.scalar.activation(out=o[:, cols], in_=y[:, cols], func=GELU)
-            nc.sync.dma_start(out=out[i * P : (i + 1) * P, cols], in_=o[:, cols])
+        def add(i, n0=0, n1=N):
+            nc.vector.tensor_tensor(out=y[:, i * N + n0 : i * N + n1], in0=accs[i][:, n0:n1], in1=bias[:, n0:n1], op=ADD)
 
-        copy(0, "V")
-        quantize(0)
-        nc.scalar.copy(out=bias[:].rearrange("t (p m) -> t p m", m=4), in_=b_ps[:].rearrange("t m p -> t p m"))
-        copy(1, "V")
-        copy(2, "S")
-        quantize(1)
-        quantize(2)
-        copy(3, "S")
-        copy(4, "G")
-        for i in range(0, TILES - 2, 2):
+        def activate(i, n0=0, n1=N):
+            nc.scalar.activation(out=o[:, i * N + n0 : i * N + n1], in_=y[:, i * N + n0 : i * N + n1], func=GELU)
+
+        def store(i, n0=0, n1=N, queue=nc.sync):
+            queue.dma_start(out=out[i * P : (i + 1) * P, n0:n1], in_=o[:, i * N + n0 : i * N + n1])
+
+        def finish(i):
+            activate(i)
+            store(i)
+
+        def place_bias():
+            nc.scalar.copy(out=bias[:].rearrange("t (p m) -> t p m", m=4), in_=b_ps[:].rearrange("t m p -> t p m"))
+
+        copy("V", 0, P)
+        quantize(0, P)
+        base_pass(0)
+        copy("V", P, P + P // 2)
+        copy("S", P + P // 2, 2 * P)
+        quantize(P, 2 * P)
+        base_pass(1)
+        spread_bias()
+        copy("V", 2 * P, 4 * P)
+        copy("S", 4 * P, 5 * P)
+        place_bias()
+        rest_pass(0)
+        rest_pass(1)
+        quantize(2 * P, 4 * P)
+        quantize(4 * P, 5 * P)
+        for i in range(2, 5):
+            multiply(i)
+        copy("G", 5 * P, 7 * P)
+        for i in (0, 1, 2):
             add(i)
             finish(i)
-            if i + 5 < TILES - 1:
-                copy(i + 5, "S")
-            add(i + 1)
-            finish(i + 1)
-            if i + 5 == TILES - 1:
-                copy(TILES - 1, "V")
-            quantize(i + 3)
-            if i + 4 < TILES:
-                quantize(i + 4)
-            if i + 6 < TILES:
-                copy(i + 6, "G")
-        add(TILES - 2)
-        finish(TILES - 2)
-        for half in (slice(0, N // 2), slice(N // 2, N)):
-            add(TILES - 1, half)
-            finish(TILES - 1, half)
+            if i < 2:
+                copy("S", (7 + i) * P, (8 + i) * P)
+        quantize(5 * P, 7 * P)
+        copy("G", 9 * P, 11 * P)
+        quantize(7 * P, 8 * P)
+        for i in (5, 6, 7):
+            multiply(i)
+        for i in (3, 4, 5):
+            add(i)
+            finish(i)
+        quantize(9 * P, 11 * P)
+        copy("G", 11 * P, 12 * P)
+        quantize(8 * P, 9 * P)
+        for i in (8, 9, 10):
+            multiply(i)
+        for i in (6, 7, 8):
+            add(i)
+            finish(i)
+        quantize(11 * P, 12 * P)
+        multiply(11)
+        for i in range(TILES - 3, TILES):
+            for n0 in (0, N // 2):
+                add(i, n0, n0 + N // 2)
+                activate(i, n0, n0 + N // 2)
+                if i == TILES - 1:
+                    store(i, n0, n0 + N // 2)
+            if i < TILES - 1:
+                store(i)

@@ -19,9 +19,11 @@ ADD = mybir.AluOpType.add
 
 P = 128
 TILES = T // P
-CHUNKS = [128, 128, 384, 256, 256, 256, 128]
 PAIR = 2 * P
-GPSIMD_SPANS = [(5 * P, 7 * P), (9 * P, 11 * P), (11 * P, 12 * P)]
+PAIRS = T // PAIR
+CHUNKS = [256, 512, 256, 256, 256]
+HEAD_SHARE = 176
+TURN_PAIRS = (2, 3, 4)
 
 
 def tile_mix_resid_tm_gelu_kernel(tc, x, w4_words, w4_scales, r8_words, r8_scales, b, out):
@@ -32,17 +34,16 @@ def tile_mix_resid_tm_gelu_kernel(tc, x, w4_words, w4_scales, r8_words, r8_scale
         psum_b = ctx.enter_context(tc.psum_pool(name="psum_b", bufs=1))
         ctx.enter_context(tc.manual_schedule())
 
-        w_planes = keep.tile([P, 2 * N], U8, align_bytes=64, name="w_planes")
-        w4_plane = w_planes[:, 0:N]
-        r8_plane = w_planes[:, N : 2 * N]
+        w4_plane = keep.tile([P, N], U8, align_bytes=64, name="w4_plane")
+        r8_plane = keep.tile([P, N], U8, align_bytes=64, name="r8_plane")
         w4 = keep.tile([P, 2 * N], U8, align_bytes=64, name="w4")
         r8 = keep.tile([P, 4 * N], U8, align_bytes=64, name="r8")
         warm = keep.tile([P, 1], F32, name="warm")
         b_cols = keep.tile([P, 4], F32, name="b_cols")
         bias = keep.tile([P, N], F32, name="bias")
         ident = keep.tile([P, P], F32, name="ident")
-        grouped = keep.tile([P, 4 * T], BF16, align_bytes=64, name="grouped")
         turn = keep.tile([P, 4 * PAIR], BF16, align_bytes=64, name="turn")
+        grouped = [turn if r in TURN_PAIRS else keep.tile([P, 4 * PAIR], BF16, align_bytes=64, name=f"grouped{r}") for r in range(PAIRS)]
         codes = keep.tile([P, T], U32, align_bytes=64, name="codes")
         x_plane = keep.tile([P, T], U8, align_bytes=64, name="x_plane")
         y = keep.tile([P, TILES * N], F32, name="y")
@@ -55,29 +56,35 @@ def tile_mix_resid_tm_gelu_kernel(tc, x, w4_words, w4_scales, r8_words, r8_scale
         def load_x(c, queue=nc.sync):
             queue.dma_start(out=raws[c][:], in_=xv[:, :, starts[c] : starts[c] + CHUNKS[c]])
 
-        def load_scales(queue, col, scales, q):
-            queue.dma_start(
-                out=w_planes[32 * q : 32 * q + 4, col : col + N].bitcast(I32),
-                in_=scales[0, 4 * q : 4 * q + 4, :].bitcast(I32),
-            )
+        def load_scales(queue, plane, scales, q):
+            queue.dma_start(out=plane[32 * q : 32 * q + 4, :].bitcast(I32), in_=scales[0, 4 * q : 4 * q + 4, :].bitcast(I32))
 
-        nc.vector.memset(w_planes[:].bitcast(I32), 0)
+        def load_w4(queue=nc.sync):
+            queue.dma_start(out=w4[:].bitcast(I32), in_=w4_words[0].bitcast(I32))
+
+        def load_r8(queue=nc.sync):
+            queue.dma_start(out=r8[:].bitcast(I32), in_=r8_words[0].rearrange("p n i -> p (n i)").bitcast(I32))
+
+        def load_b(queue=nc.sync):
+            queue.dma_start(out=b_cols[:], in_=b.rearrange("(p m) -> p m", m=4))
+
+        nc.gpsimd.memset(w4_plane[:].bitcast(I32), 0)
+        nc.vector.memset(r8_plane[:].bitcast(I32), 0)
         nc.vector.memset(ident[:], 0.0)
         nc.vector.memset(warm[:], 0.0)
         nc.scalar.activation(out=warm[:], in_=warm[:], func=GELU)
         make_identity(nc, ident[:], nomemset=True)
 
         load_x(0)
+        load_w4()
+        load_b()
         for q in range(4):
-            load_scales(nc.sync, 0, w4_scales, q)
-        nc.sync.dma_start(out=w4[:].bitcast(I32), in_=w4_words[0].bitcast(I32))
+            load_scales(nc.sync, w4_plane, w4_scales, q)
         load_x(1)
-        load_x(2)
-        nc.sync.dma_start(out=b_cols[:], in_=b.rearrange("(p m) -> p m", m=4))
-        nc.sync.dma_start(out=r8[:].bitcast(I32), in_=r8_words[0].rearrange("p n i -> p (n i)").bitcast(I32))
+        load_r8()
         for q in range(4):
-            load_scales(nc.sync, N, r8_scales, q)
-        for c in range(3, len(CHUNKS)):
+            load_scales(nc.sync, r8_plane, r8_scales, q)
+        for c in range(2, len(CHUNKS)):
             load_x(c)
 
         b_ps = psum_b.tile([P, 4, P], F32, name="b_ps")
@@ -86,17 +93,16 @@ def tile_mix_resid_tm_gelu_kernel(tc, x, w4_words, w4_scales, r8_words, r8_scale
             for m in range(4):
                 nc.tensor.transpose(b_ps[:, m, :], b_cols[:, m : m + 1].to_broadcast([P, P]), ident[:])
 
+        def place_bias():
+            nc.scalar.copy(out=bias[:].rearrange("t (p m) -> t p m", m=4), in_=b_ps[:].rearrange("t m p -> t p m"))
+
         accs = {}
 
-        def staged(t0, t1):
-            if (t0, t1) in GPSIMD_SPANS:
-                return turn[:, 0 : 4 * (t1 - t0)]
-            return grouped[:, 4 * t0 : 4 * t1]
-
-        def copy(engine, t0, t1):
+        def copy(engine, pair, lo=0, hi=PAIR):
+            t0 = pair * PAIR + lo
             c = max(j for j in range(len(CHUNKS)) if starts[j] <= t0)
-            src = raws[c][:, :, t0 - starts[c] : t1 - starts[c]]
-            dst = staged(t0, t1)
+            src = raws[c][:, :, t0 - starts[c] : t0 - starts[c] + hi - lo]
+            dst = grouped[pair][:, 4 * lo : 4 * hi]
             if engine == "G":
                 nc.gpsimd.tensor_scalar(out=dst.rearrange("p (w j) -> p w j", j=4), in0=src.rearrange("p j w -> p w j"),
                                         scalar1=1.0, scalar2=0.0, op0=MULT, op1=ADD)
@@ -108,24 +114,26 @@ def tile_mix_resid_tm_gelu_kernel(tc, x, w4_words, w4_scales, r8_words, r8_scale
             else:
                 nc.scalar.copy(out=dst, in_=src)
 
-        def quantize(t0, t1):
-            nc.vector.quantize_mx(out=codes[:, t0:t1].bitcast(FP8X4), scales=x_plane[:, t0:t1], in_=staged(t0, t1))
+        def quantize(pair):
+            cols = slice(pair * PAIR, (pair + 1) * PAIR)
+            nc.vector.quantize_mx(out=codes[:, cols].bitcast(FP8X4), scales=x_plane[:, cols], in_=grouped[pair][:])
 
         def base_pass(i):
             acc = psum.tile([P, N], F32, name="acc")
             accs[i] = acc
             cols = slice(i * P, (i + 1) * P)
             nc.tensor.matmul_mx(out=acc[:], lhsT=codes[:, cols].bitcast(FP8X4), lhsT_scale=x_plane[:, cols],
-                                rhs=w4[:].bitcast(FP4X4), rhs_scale=w4_plane, start=True, stop=False)
+                                rhs=w4[:].bitcast(FP4X4), rhs_scale=w4_plane[:], start=True, stop=False)
 
         def rest_pass(i):
             cols = slice(i * P, (i + 1) * P)
             nc.tensor.matmul_mx(out=accs[i][:], lhsT=codes[:, cols].bitcast(FP8X4), lhsT_scale=x_plane[:, cols],
-                                rhs=r8[:].bitcast(FP8X4), rhs_scale=r8_plane, start=False, stop=True)
+                                rhs=r8[:].bitcast(FP8X4), rhs_scale=r8_plane[:], start=False, stop=True)
 
-        def multiply(i):
-            base_pass(i)
-            rest_pass(i)
+        def multiply(pair):
+            for i in (2 * pair, 2 * pair + 1):
+                base_pass(i)
+                rest_pass(i)
 
         def add(i, n0=0, n1=N):
             nc.vector.tensor_tensor(out=y[:, i * N + n0 : i * N + n1], in0=accs[i][:, n0:n1], in1=bias[:, n0:n1], op=ADD)
@@ -136,59 +144,45 @@ def tile_mix_resid_tm_gelu_kernel(tc, x, w4_words, w4_scales, r8_words, r8_scale
         def store(i, n0=0, n1=N, queue=nc.sync):
             queue.dma_start(out=out[i * P : (i + 1) * P, n0:n1], in_=o[:, i * N + n0 : i * N + n1])
 
+        copy("V", 0, 0, HEAD_SHARE)
+        copy("S", 0, HEAD_SHARE, PAIR)
+        spread_bias()
+        place_bias()
+        quantize(0)
+        base_pass(0)
+        base_pass(1)
+        copy("V", 1)
+        copy("S", 2, PAIR - HEAD_SHARE, PAIR)
+        rest_pass(0)
+        rest_pass(1)
+        copy("V", 2, 0, PAIR - HEAD_SHARE)
+        quantize(1)
+        multiply(1)
+
         def finish(i):
+            add(i)
             activate(i)
             store(i)
 
-        def place_bias():
-            nc.scalar.copy(out=bias[:].rearrange("t (p m) -> t p m", m=4), in_=b_ps[:].rearrange("t m p -> t p m"))
-
-        copy("V", 0, P)
-        quantize(0, P)
-        base_pass(0)
-        copy("V", P, P + P // 2)
-        copy("S", P + P // 2, 2 * P)
-        quantize(P, 2 * P)
-        base_pass(1)
-        spread_bias()
-        copy("V", 2 * P, 4 * P)
-        copy("S", 4 * P, 5 * P)
-        place_bias()
-        rest_pass(0)
-        rest_pass(1)
-        quantize(2 * P, 4 * P)
-        quantize(4 * P, 5 * P)
-        for i in range(2, 5):
-            multiply(i)
-        copy("G", 5 * P, 7 * P)
-        for i in (0, 1, 2):
-            add(i)
+        finish(0)
+        quantize(2)
+        multiply(2)
+        copy("G", 3)
+        for i in (1, 2, 3):
             finish(i)
-            if i < 2:
-                copy("S", (7 + i) * P, (8 + i) * P)
-        quantize(5 * P, 7 * P)
-        copy("G", 9 * P, 11 * P)
-        quantize(7 * P, 8 * P)
-        for i in (5, 6, 7):
-            multiply(i)
-        for i in (3, 4, 5):
-            add(i)
+        quantize(3)
+        multiply(3)
+        copy("G", 4)
+        copy("S", 5)
+        for i in (4, 5, 6):
             finish(i)
-        quantize(9 * P, 11 * P)
-        copy("G", 11 * P, 12 * P)
-        quantize(8 * P, 9 * P)
-        for i in (8, 9, 10):
-            multiply(i)
-        for i in (6, 7, 8):
-            add(i)
+        for pair in (4, 5):
+            quantize(pair)
+            multiply(pair)
+        for i in (7, 8):
             finish(i)
-        quantize(11 * P, 12 * P)
-        multiply(11)
-        for i in range(TILES - 3, TILES):
+        for i in (9, 10, 11):
             for n0 in (0, N // 2):
                 add(i, n0, n0 + N // 2)
                 activate(i, n0, n0 + N // 2)
-                if i == TILES - 1:
-                    store(i, n0, n0 + N // 2)
-            if i < TILES - 1:
-                store(i)
+            store(i)

@@ -24,6 +24,7 @@ PAIRS = T // PAIR
 CHUNKS = [256, 512, 256, 256, 256]
 HEAD_SHARE = 176
 TURN_PAIRS = (2, 3, 4)
+GPSIMD_SHARE = 160
 
 
 def tile_mix_resid_tm_gelu_kernel(tc, x, w4_words, w4_scales, r8_words, r8_scales, b, out):
@@ -136,7 +137,7 @@ def tile_mix_resid_tm_gelu_kernel(tc, x, w4_words, w4_scales, r8_words, r8_scale
                 rest_pass(i)
 
         def add(i, n0=0, n1=N):
-            nc.vector.tensor_tensor(out=y[:, i * N + n0 : i * N + n1], in0=accs[i][:, n0:n1], in1=bias[:, n0:n1], op=ADD)
+            nc.vector.tensor_tensor(out=y[:, i * N + n0 : i * N + n1], in0=bias[:, n0:n1], in1=accs[i][:, n0:n1], op=ADD)
 
         def activate(i, n0=0, n1=N):
             nc.scalar.activation(out=o[:, i * N + n0 : i * N + n1], in_=y[:, i * N + n0 : i * N + n1], func=GELU)
@@ -167,13 +168,17 @@ def tile_mix_resid_tm_gelu_kernel(tc, x, w4_words, w4_scales, r8_words, r8_scale
         finish(0)
         quantize(2)
         multiply(2)
-        copy("G", 3)
-        for i in (1, 2, 3):
+        copy("G", 3, 0, GPSIMD_SHARE)
+        copy("S", 3, GPSIMD_SHARE, PAIR)
+        for i in (1, 2):
             finish(i)
+        copy("S", 5, P, PAIR)
+        finish(3)
         quantize(3)
         multiply(3)
-        copy("G", 4)
-        copy("S", 5)
+        copy("V", 5, 0, P)
+        copy("G", 4, 0, GPSIMD_SHARE)
+        copy("S", 4, GPSIMD_SHARE, PAIR)
         for i in (4, 5, 6):
             finish(i)
         for pair in (4, 5):
@@ -185,4 +190,7 @@ def tile_mix_resid_tm_gelu_kernel(tc, x, w4_words, w4_scales, r8_words, r8_scale
             for n0 in (0, N // 2):
                 add(i, n0, n0 + N // 2)
                 activate(i, n0, n0 + N // 2)
-            store(i)
+                if i == TILES - 1:
+                    store(i, n0, n0 + N // 2)
+            if i < TILES - 1:
+                store(i)

@@ -24,7 +24,6 @@ PAIRS = T // PAIR
 CHUNKS = [256, 512, 256, 256, 256]
 HEAD_SHARE = 176
 TURN_PAIRS = (2, 3, 4)
-GPSIMD_SHARE = 160
 
 
 def tile_mix_resid_tm_gelu_kernel(tc, x, w4_words, w4_scales, r8_words, r8_scales, b, out):
@@ -115,9 +114,9 @@ def tile_mix_resid_tm_gelu_kernel(tc, x, w4_words, w4_scales, r8_words, r8_scale
             else:
                 nc.scalar.copy(out=dst, in_=src)
 
-        def quantize(pair):
-            cols = slice(pair * PAIR, (pair + 1) * PAIR)
-            nc.vector.quantize_mx(out=codes[:, cols].bitcast(FP8X4), scales=x_plane[:, cols], in_=grouped[pair][:])
+        def quantize(pair, lo=0, hi=PAIR):
+            cols = slice(pair * PAIR + lo, pair * PAIR + hi)
+            nc.vector.quantize_mx(out=codes[:, cols].bitcast(FP8X4), scales=x_plane[:, cols], in_=grouped[pair][:, 4 * lo : 4 * hi])
 
         def base_pass(i):
             acc = psum.tile([P, N], F32, name="acc")
@@ -152,45 +151,42 @@ def tile_mix_resid_tm_gelu_kernel(tc, x, w4_words, w4_scales, r8_words, r8_scale
         quantize(0)
         base_pass(0)
         base_pass(1)
-        copy("V", 1)
-        copy("S", 2, PAIR - HEAD_SHARE, PAIR)
+        copy("V", 1, 0, HEAD_SHARE)
+        copy("S", 1, HEAD_SHARE, PAIR)
+        copy("V", 2, 0, P)
+        copy("S", 2, P, PAIR)
         rest_pass(0)
         rest_pass(1)
-        copy("V", 2, 0, PAIR - HEAD_SHARE)
-        quantize(1)
-        multiply(1)
+        for pair in (1, 2):
+            quantize(pair)
+            multiply(pair)
 
         def finish(i):
             add(i)
             activate(i)
             store(i)
 
+        copy("G", 3, 0, 192)
         finish(0)
-        quantize(2)
-        multiply(2)
-        copy("G", 3, 0, GPSIMD_SHARE)
-        copy("S", 3, GPSIMD_SHARE, PAIR)
-        for i in (1, 2):
+        copy("S", 3, 192, PAIR)
+        for i in (1, 2, 3):
             finish(i)
-        copy("S", 5, P, PAIR)
-        finish(3)
         quantize(3)
         multiply(3)
-        copy("V", 5, 0, P)
-        copy("G", 4, 0, GPSIMD_SHARE)
-        copy("S", 4, GPSIMD_SHARE, PAIR)
-        for i in (4, 5, 6):
+        copy("G", 4, 0, 160)
+        copy("S", 4, 160, PAIR)
+        finish(4)
+        copy("S", 5, 192, PAIR)
+        for i in (5, 6):
             finish(i)
-        for pair in (4, 5):
-            quantize(pair)
-            multiply(pair)
-        for i in (7, 8):
-            finish(i)
-        for i in (9, 10, 11):
+        quantize(4)
+        multiply(4)
+        copy("V", 5, 0, 192)
+        finish(7)
+        quantize(5)
+        multiply(5)
+        for i in range(8, TILES):
             for n0 in (0, N // 2):
                 add(i, n0, n0 + N // 2)
                 activate(i, n0, n0 + N // 2)
-                if i == TILES - 1:
-                    store(i, n0, n0 + N // 2)
-            if i < TILES - 1:
-                store(i)
+                store(i, n0, n0 + N // 2)

@@ -151,6 +151,11 @@ def tile_mix_resid_tm_gelu_kernel(tc, x, w4_words, w4_scales, r8_words, r8_scale
         quantize(0)
         base_pass(0)
         base_pass(1)
+        idle = psum.tile([P, N], F32, name="acc")
+        for i in (0, 1):
+            cols = slice(i * P, (i + 1) * P)
+            nc.tensor.matmul_mx(out=idle[:], lhsT=codes[:, cols].bitcast(FP8X4), lhsT_scale=x_plane[:, cols],
+                                rhs=w4[:].bitcast(FP4X4), rhs_scale=w4_plane[:], start=True, stop=True)
         copy("V", 1, 0, HEAD_SHARE)
         copy("S", 1, HEAD_SHARE, PAIR)
         copy("V", 2, 0, P)

@@ -21,16 +21,24 @@ P = 128
 TILES = T // P
 PAIR = 2 * P
 PAIRS = T // PAIR
-CHUNKS = [256, 512, 256, 256, 256]
-HEAD_SHARE = 176
+HALF = N // 2
+HALVES = ((0, HALF), (HALF, N))
+CHUNKS = [PAIR, 2 * PAIR, PAIR, PAIR, PAIR]
 TURN_PAIRS = (2, 3, 4)
+VECTOR_HEAD = 176
+VECTOR_PAIR_2 = 128
+GPSIMD_PAIR_3 = 192
+GPSIMD_PAIR_4 = 160
+VECTOR_PAIR_5 = 192
+LAST_RUN = 8
+SUM_BANKS = 7
 
 
 def tile_mix_resid_tm_gelu_kernel(tc, x, w4_words, w4_scales, r8_words, r8_scales, b, out):
     nc = tc.nc
     with ExitStack() as ctx:
         keep = ctx.enter_context(tc.tile_pool(name="keep", bufs=1))
-        psum = ctx.enter_context(tc.psum_pool(name="psum", bufs=7))
+        psum = ctx.enter_context(tc.psum_pool(name="psum", bufs=SUM_BANKS))
         psum_b = ctx.enter_context(tc.psum_pool(name="psum_b", bufs=1))
         ctx.enter_context(tc.manual_schedule())
 
@@ -53,20 +61,12 @@ def tile_mix_resid_tm_gelu_kernel(tc, x, w4_words, w4_scales, r8_words, r8_scale
         starts = [sum(CHUNKS[:c]) for c in range(len(CHUNKS))]
         raws = [keep.tile([P, 4, w], F32, name=f"raw{c}") for c, w in enumerate(CHUNKS)]
 
-        def load_x(c, queue=nc.sync):
-            queue.dma_start(out=raws[c][:], in_=xv[:, :, starts[c] : starts[c] + CHUNKS[c]])
+        def load_x(c):
+            nc.sync.dma_start(out=raws[c][:], in_=xv[:, :, starts[c] : starts[c] + CHUNKS[c]])
 
-        def load_scales(queue, plane, scales, q):
-            queue.dma_start(out=plane[32 * q : 32 * q + 4, :].bitcast(I32), in_=scales[0, 4 * q : 4 * q + 4, :].bitcast(I32))
-
-        def load_w4(queue=nc.sync):
-            queue.dma_start(out=w4[:].bitcast(I32), in_=w4_words[0].bitcast(I32))
-
-        def load_r8(queue=nc.sync):
-            queue.dma_start(out=r8[:].bitcast(I32), in_=r8_words[0].rearrange("p n i -> p (n i)").bitcast(I32))
-
-        def load_b(queue=nc.sync):
-            queue.dma_start(out=b_cols[:], in_=b.rearrange("(p m) -> p m", m=4))
+        def load_scales(plane, scales):
+            for r in range(4):
+                nc.sync.dma_start(out=plane[r:P:32, :].bitcast(I32), in_=scales[0, r:16:4, :].bitcast(I32))
 
         nc.gpsimd.memset(w4_plane[:].bitcast(I32), 0)
         nc.vector.memset(r8_plane[:].bitcast(I32), 0)
@@ -76,122 +76,126 @@ def tile_mix_resid_tm_gelu_kernel(tc, x, w4_words, w4_scales, r8_words, r8_scale
         make_identity(nc, ident[:], nomemset=True)
 
         load_x(0)
-        load_w4()
-        load_b()
-        for q in range(4):
-            load_scales(nc.sync, w4_plane, w4_scales, q)
+        nc.sync.dma_start(out=w4[:].bitcast(I32), in_=w4_words[0].bitcast(I32))
+        nc.sync.dma_start(out=b_cols[:], in_=b.rearrange("(p m) -> p m", m=4))
+        load_scales(w4_plane, w4_scales)
         load_x(1)
-        load_r8()
-        for q in range(4):
-            load_scales(nc.sync, r8_plane, r8_scales, q)
+        nc.sync.dma_start(out=r8[:].bitcast(I32), in_=r8_words[0].rearrange("p n i -> p (n i)").bitcast(I32))
+        load_scales(r8_plane, r8_scales)
         for c in range(2, len(CHUNKS)):
             load_x(c)
 
         b_ps = psum_b.tile([P, 4, P], F32, name="b_ps")
+        sums = {}
 
         def spread_bias():
             for m in range(4):
                 nc.tensor.transpose(b_ps[:, m, :], b_cols[:, m : m + 1].to_broadcast([P, P]), ident[:])
-
-        def place_bias():
             nc.scalar.copy(out=bias[:].rearrange("t (p m) -> t p m", m=4), in_=b_ps[:].rearrange("t m p -> t p m"))
 
-        accs = {}
-
-        def copy(engine, pair, lo=0, hi=PAIR):
+        def sides(pair, lo, hi):
             t0 = pair * PAIR + lo
             c = max(j for j in range(len(CHUNKS)) if starts[j] <= t0)
-            src = raws[c][:, :, t0 - starts[c] : t0 - starts[c] + hi - lo]
-            dst = grouped[pair][:, 4 * lo : 4 * hi]
-            if engine == "G":
-                nc.gpsimd.tensor_scalar(out=dst.rearrange("p (w j) -> p w j", j=4), in0=src.rearrange("p j w -> p w j"),
-                                        scalar1=1.0, scalar2=0.0, op0=MULT, op1=ADD)
-                return
-            dst = dst.rearrange("p (c i j) -> p c j i", i=4, j=4)
-            src = src.rearrange("p j (c i) -> p c j i", i=4)
-            if engine == "V":
-                nc.vector.tensor_copy(out=dst, in_=src)
-            else:
-                nc.scalar.copy(out=dst, in_=src)
+            return raws[c][:, :, t0 - starts[c] : t0 - starts[c] + hi - lo], grouped[pair][:, 4 * lo : 4 * hi]
 
-        def quantize(pair, lo=0, hi=PAIR):
-            cols = slice(pair * PAIR + lo, pair * PAIR + hi)
-            nc.vector.quantize_mx(out=codes[:, cols].bitcast(FP8X4), scales=x_plane[:, cols], in_=grouped[pair][:, 4 * lo : 4 * hi])
+        def copy_by_fours(copy, pair, lo, hi):
+            src, dst = sides(pair, lo, hi)
+            copy(out=dst.rearrange("p (c i j) -> p c j i", i=4, j=4), in_=src.rearrange("p j (c i) -> p c j i", i=4))
 
-        def base_pass(i):
-            acc = psum.tile([P, N], F32, name="acc")
-            accs[i] = acc
+        def copy_gpsimd(pair, lo, hi):
+            src, dst = sides(pair, lo, hi)
+            nc.gpsimd.tensor_scalar(out=dst.rearrange("p (w j) -> p w j", j=4), in0=src.rearrange("p j w -> p w j"),
+                                    scalar1=1.0, scalar2=0.0, op0=MULT, op1=ADD)
+
+        def quantize(pair):
+            cols = slice(pair * PAIR, (pair + 1) * PAIR)
+            nc.vector.quantize_mx(out=codes[:, cols].bitcast(FP8X4), scales=x_plane[:, cols], in_=grouped[pair][:])
+
+        def w4_pass(acc, i, n0, n1, start, stop):
             cols = slice(i * P, (i + 1) * P)
-            nc.tensor.matmul_mx(out=acc[:], lhsT=codes[:, cols].bitcast(FP8X4), lhsT_scale=x_plane[:, cols],
-                                rhs=w4[:].bitcast(FP4X4), rhs_scale=w4_plane[:], start=True, stop=False)
+            nc.tensor.matmul_mx(out=acc, lhsT=codes[:, cols].bitcast(FP8X4), lhsT_scale=x_plane[:, cols],
+                                rhs=w4[:, 2 * n0 : 2 * n1].bitcast(FP4X4), rhs_scale=w4_plane[:, n0:n1], start=start, stop=stop)
 
-        def rest_pass(i):
+        def r8_pass(acc, i, n0, n1):
             cols = slice(i * P, (i + 1) * P)
-            nc.tensor.matmul_mx(out=accs[i][:], lhsT=codes[:, cols].bitcast(FP8X4), lhsT_scale=x_plane[:, cols],
-                                rhs=r8[:].bitcast(FP8X4), rhs_scale=r8_plane[:], start=False, stop=True)
+            nc.tensor.matmul_mx(out=acc, lhsT=codes[:, cols].bitcast(FP8X4), lhsT_scale=x_plane[:, cols],
+                                rhs=r8[:, 4 * n0 : 4 * n1].bitcast(FP8X4), rhs_scale=r8_plane[:, n0:n1], start=False, stop=True)
+
+        def open_sum(i):
+            sums[i] = psum.tile([P, N], F32, name="acc")
+            w4_pass(sums[i][:], i, 0, N, start=True, stop=False)
+
+        def close_sum(i):
+            r8_pass(sums[i][:], i, 0, N)
 
         def multiply(pair):
             for i in (2 * pair, 2 * pair + 1):
-                base_pass(i)
-                rest_pass(i)
+                open_sum(i)
+                close_sum(i)
 
-        def add(i, n0=0, n1=N):
-            nc.vector.tensor_tensor(out=y[:, i * N + n0 : i * N + n1], in0=bias[:, n0:n1], in1=accs[i][:, n0:n1], op=ADD)
+        def add_and_activate(acc, i, n0, n1):
+            cols = slice(i * N + n0, i * N + n1)
+            nc.vector.tensor_tensor(out=y[:, cols], in0=bias[:, n0:n1], in1=acc, op=ADD)
+            nc.scalar.activation(out=o[:, cols], in_=y[:, cols], func=GELU)
 
-        def activate(i, n0=0, n1=N):
-            nc.scalar.activation(out=o[:, i * N + n0 : i * N + n1], in_=y[:, i * N + n0 : i * N + n1], func=GELU)
+        def store(i, n0, n1):
+            nc.sync.dma_start(out=out[i * P : (i + 1) * P, n0:n1], in_=o[:, i * N + n0 : i * N + n1])
 
-        def store(i, n0=0, n1=N, queue=nc.sync):
-            queue.dma_start(out=out[i * P : (i + 1) * P, n0:n1], in_=o[:, i * N + n0 : i * N + n1])
+        def finish(i):
+            add_and_activate(sums[i][:], i, 0, N)
+            store(i, 0, N)
 
-        copy("V", 0, 0, HEAD_SHARE)
-        copy("S", 0, HEAD_SHARE, PAIR)
+        first_sums = [psum.tile([P, N], F32, name="acc") for h in range(2)]
+
+        copy_by_fours(nc.vector.tensor_copy, 0, 0, VECTOR_HEAD)
+        copy_by_fours(nc.scalar.copy, 0, VECTOR_HEAD, PAIR)
         spread_bias()
-        place_bias()
         quantize(0)
-        base_pass(0)
-        base_pass(1)
-        idle = psum.tile([P, N], F32, name="acc")
+        for acc, (n0, n1) in zip(first_sums, HALVES):
+            w4_pass(acc[:, :P], 0, n0, n0 + P, start=True, stop=False)
+            w4_pass(acc[:, P:HALF], 0, n0 + P, n1, start=False, stop=False)
+        open_sum(1)
+        unread = psum.tile([P, N], F32, name="acc")
         for i in (0, 1):
-            cols = slice(i * P, (i + 1) * P)
-            nc.tensor.matmul_mx(out=idle[:], lhsT=codes[:, cols].bitcast(FP8X4), lhsT_scale=x_plane[:, cols],
-                                rhs=w4[:].bitcast(FP4X4), rhs_scale=w4_plane[:], start=True, stop=True)
-        copy("V", 1, 0, HEAD_SHARE)
-        copy("S", 1, HEAD_SHARE, PAIR)
-        copy("V", 2, 0, P)
-        copy("S", 2, P, PAIR)
-        rest_pass(0)
-        rest_pass(1)
+            w4_pass(unread[:], i, 0, N, start=True, stop=True)
+        copy_by_fours(nc.vector.tensor_copy, 1, 0, VECTOR_HEAD)
+        copy_by_fours(nc.scalar.copy, 1, VECTOR_HEAD, PAIR)
+        copy_by_fours(nc.vector.tensor_copy, 2, 0, VECTOR_PAIR_2)
+        copy_by_fours(nc.scalar.copy, 2, VECTOR_PAIR_2, PAIR)
+        for acc, (n0, n1) in zip(first_sums, HALVES):
+            r8_pass(acc[:, :HALF], 0, n0, n1)
+        close_sum(1)
         for pair in (1, 2):
             quantize(pair)
             multiply(pair)
 
-        def finish(i):
-            add(i)
-            activate(i)
-            store(i)
-
-        copy("G", 3, 0, 192)
-        finish(0)
-        copy("S", 3, 192, PAIR)
+        copy_gpsimd(3, 0, GPSIMD_PAIR_3)
+        for acc, (n0, n1) in zip(first_sums, HALVES):
+            add_and_activate(acc[:, :HALF], 0, n0, n1)
+        store(0, 0, N)
+        copy_by_fours(nc.scalar.copy, 3, GPSIMD_PAIR_3, PAIR)
         for i in (1, 2, 3):
             finish(i)
         quantize(3)
         multiply(3)
-        copy("G", 4, 0, 160)
-        copy("S", 4, 160, PAIR)
+
+        copy_gpsimd(4, 0, GPSIMD_PAIR_4)
+        copy_by_fours(nc.scalar.copy, 4, GPSIMD_PAIR_4, PAIR)
         finish(4)
-        copy("S", 5, 192, PAIR)
+        copy_by_fours(nc.scalar.copy, 5, VECTOR_PAIR_5, PAIR)
         for i in (5, 6):
             finish(i)
         quantize(4)
         multiply(4)
-        copy("V", 5, 0, 192)
-        finish(7)
+
+        copy_by_fours(nc.vector.tensor_copy, 5, 0, VECTOR_PAIR_5)
+        for n0, n1 in HALVES:
+            add_and_activate(sums[LAST_RUN - 1][:, n0:n1], LAST_RUN - 1, n0, n1)
+        store(LAST_RUN - 1, 0, N)
         quantize(5)
         multiply(5)
-        for i in range(8, TILES):
-            for n0 in (0, N // 2):
-                add(i, n0, n0 + N // 2)
-                activate(i, n0, n0 + N // 2)
-                store(i, n0, n0 + N // 2)
+
+        for i in range(LAST_RUN, TILES):
+            for n0, n1 in HALVES:
+                add_and_activate(sums[i][:, n0:n1], i, n0, n1)
+                store(i, n0, n1)

@@ -23,14 +23,9 @@ PAIR = 2 * P
 PAIRS = T // PAIR
 HALF = N // 2
 HALVES = ((0, HALF), (HALF, N))
-CHUNKS = [PAIR, 2 * PAIR, PAIR, PAIR, PAIR]
-TURN_PAIRS = (2, 3, 4)
-VECTOR_HEAD = 176
-VECTOR_PAIR_2 = 128
-GPSIMD_PAIR_3 = 192
-GPSIMD_PAIR_4 = 160
-VECTOR_PAIR_5 = 192
-LAST_RUN = 8
+CHUNKS = [PAIR] * PAIRS
+GATED = [3,4,5]
+OVERLAP = 8
 SUM_BANKS = 7
 
 
@@ -50,8 +45,9 @@ def tile_mix_resid_tm_gelu_kernel(tc, x, w4_words, w4_scales, r8_words, r8_scale
         b_cols = keep.tile([P, 4], F32, name="b_cols")
         bias = keep.tile([P, N], F32, name="bias")
         ident = keep.tile([P, P], F32, name="ident")
-        turn = keep.tile([P, 4 * PAIR], BF16, align_bytes=64, name="turn")
-        grouped = [turn if r in TURN_PAIRS else keep.tile([P, 4 * PAIR], BF16, align_bytes=64, name=f"grouped{r}") for r in range(PAIRS)]
+        staged = keep.tile([P, 4 * T], BF16, align_bytes=64, name="staged")
+        first_token = [r * PAIR - OVERLAP * len([g for g in GATED if g <= r]) for r in range(PAIRS)]
+        grouped = [staged[:, 4 * t : 4 * (t + PAIR)] for t in first_token]
         codes = keep.tile([P, T], U32, align_bytes=64, name="codes")
         x_plane = keep.tile([P, T], U8, align_bytes=64, name="x_plane")
         y = keep.tile([P, TILES * N], F32, name="y")
@@ -76,8 +72,8 @@ def tile_mix_resid_tm_gelu_kernel(tc, x, w4_words, w4_scales, r8_words, r8_scale
         make_identity(nc, ident[:], nomemset=True)
 
         load_x(0)
-        nc.sync.dma_start(out=w4[:].bitcast(I32), in_=w4_words[0].bitcast(I32))
         nc.sync.dma_start(out=b_cols[:], in_=b.rearrange("(p m) -> p m", m=4))
+        nc.sync.dma_start(out=w4[:].bitcast(I32), in_=w4_words[0].bitcast(I32))
         load_scales(w4_plane, w4_scales)
         load_x(1)
         nc.sync.dma_start(out=r8[:].bitcast(I32), in_=r8_words[0].rearrange("p n i -> p (n i)").bitcast(I32))
@@ -107,9 +103,9 @@ def tile_mix_resid_tm_gelu_kernel(tc, x, w4_words, w4_scales, r8_words, r8_scale
             nc.gpsimd.tensor_scalar(out=dst.rearrange("p (w j) -> p w j", j=4), in0=src.rearrange("p j w -> p w j"),
                                     scalar1=1.0, scalar2=0.0, op0=MULT, op1=ADD)
 
-        def quantize(pair):
-            cols = slice(pair * PAIR, (pair + 1) * PAIR)
-            nc.vector.quantize_mx(out=codes[:, cols].bitcast(FP8X4), scales=x_plane[:, cols], in_=grouped[pair][:])
+        def quantize(pair, lo=0, hi=PAIR):
+            cols = slice(pair * PAIR + lo, pair * PAIR + hi)
+            nc.vector.quantize_mx(out=codes[:, cols].bitcast(FP8X4), scales=x_plane[:, cols], in_=grouped[pair][:, 4 * lo : 4 * hi])
 
         def w4_pass(acc, i, n0, n1, start, stop):
             cols = slice(i * P, (i + 1) * P)
@@ -133,69 +129,106 @@ def tile_mix_resid_tm_gelu_kernel(tc, x, w4_words, w4_scales, r8_words, r8_scale
                 open_sum(i)
                 close_sum(i)
 
-        def add_and_activate(acc, i, n0, n1):
+        def add(acc, i, n0, n1):
+            nc.vector.tensor_tensor(out=y[:, i * N + n0 : i * N + n1], in0=bias[:, n0:n1], in1=acc, op=ADD)
+
+        def activate(i, n0, n1):
             cols = slice(i * N + n0, i * N + n1)
-            nc.vector.tensor_tensor(out=y[:, cols], in0=bias[:, n0:n1], in1=acc, op=ADD)
             nc.scalar.activation(out=o[:, cols], in_=y[:, cols], func=GELU)
 
         def store(i, n0, n1):
             nc.sync.dma_start(out=out[i * P : (i + 1) * P, n0:n1], in_=o[:, i * N + n0 : i * N + n1])
 
+        def store_tiles(i, count):
+            nc.sync.dma_start(out=out[i * P : (i + count) * P, :].rearrange("(c p) n -> p c n", p=P),
+                              in_=o[:, i * N : (i + count) * N].rearrange("p (c n) -> p c n", n=N))
+
         def finish(i):
-            add_and_activate(sums[i][:], i, 0, N)
+            add(sums[i][:], i, 0, N)
+            activate(i, 0, N)
             store(i, 0, N)
 
         first_sums = [psum.tile([P, N], F32, name="acc") for h in range(2)]
-
-        copy_by_fours(nc.vector.tensor_copy, 0, 0, VECTOR_HEAD)
-        copy_by_fours(nc.scalar.copy, 0, VECTOR_HEAD, PAIR)
+        copy_by_fours(nc.vector.tensor_copy, 0, 0, 176)
+        copy_by_fours(nc.scalar.copy, 0, 176, 256)
         spread_bias()
         quantize(0)
         for acc, (n0, n1) in zip(first_sums, HALVES):
-            w4_pass(acc[:, :P], 0, n0, n0 + P, start=True, stop=False)
-            w4_pass(acc[:, P:HALF], 0, n0 + P, n1, start=False, stop=False)
+            w4_pass(acc[:, :HALF], 0, n0, n1, start=True, stop=False)
         open_sum(1)
-        unread = psum.tile([P, N], F32, name="acc")
-        for i in (0, 1):
-            w4_pass(unread[:], i, 0, N, start=True, stop=True)
-        copy_by_fours(nc.vector.tensor_copy, 1, 0, VECTOR_HEAD)
-        copy_by_fours(nc.scalar.copy, 1, VECTOR_HEAD, PAIR)
-        copy_by_fours(nc.vector.tensor_copy, 2, 0, VECTOR_PAIR_2)
-        copy_by_fours(nc.scalar.copy, 2, VECTOR_PAIR_2, PAIR)
+        copy_by_fours(nc.vector.tensor_copy, 1, 0, 176)
+        copy_by_fours(nc.scalar.copy, 1, 176, 256)
+        quantize(1)
         for acc, (n0, n1) in zip(first_sums, HALVES):
             r8_pass(acc[:, :HALF], 0, n0, n1)
         close_sum(1)
-        for pair in (1, 2):
-            quantize(pair)
-            multiply(pair)
-
-        copy_gpsimd(3, 0, GPSIMD_PAIR_3)
-        for acc, (n0, n1) in zip(first_sums, HALVES):
-            add_and_activate(acc[:, :HALF], 0, n0, n1)
-        store(0, 0, N)
-        copy_by_fours(nc.scalar.copy, 3, GPSIMD_PAIR_3, PAIR)
-        for i in (1, 2, 3):
-            finish(i)
+        multiply(1)
+        add(first_sums[0][:, :HALF], 0, 0, HALF)
+        add(first_sums[1][:, :HALF], 0, HALF, N)
+        copy_by_fours(nc.scalar.copy, 2, 128, 256)
+        activate(0, 0, 512)
+        copy_by_fours(nc.vector.tensor_copy, 2, 0, 128)
+        add(sums[1][:, 0:512], 1, 0, 512)
+        quantize(2)
+        multiply(2)
+        copy_gpsimd(3, 0, 80)
+        copy_by_fours(nc.vector.tensor_copy, 3, 80, 144)
+        copy_by_fours(nc.scalar.copy, 3, 144, 256)
+        activate(1, 0, 512)
+        store_tiles(0, 2)
+        add(sums[2][:, 0:512], 2, 0, 512)
+        activate(2, 0, 512)
+        store(2, 0, 512)
+        add(sums[3][:, 0:512], 3, 0, 512)
         quantize(3)
         multiply(3)
-
-        copy_gpsimd(4, 0, GPSIMD_PAIR_4)
-        copy_by_fours(nc.scalar.copy, 4, GPSIMD_PAIR_4, PAIR)
-        finish(4)
-        copy_by_fours(nc.scalar.copy, 5, VECTOR_PAIR_5, PAIR)
-        for i in (5, 6):
-            finish(i)
+        copy_gpsimd(4, 0, 88)
+        copy_by_fours(nc.vector.tensor_copy, 4, 88, 152)
+        copy_by_fours(nc.scalar.copy, 4, 152, 256)
+        activate(3, 0, 512)
+        store(3, 0, 512)
+        add(sums[4][:, 0:512], 4, 0, 512)
+        activate(4, 0, 512)
+        store(4, 0, 512)
+        add(sums[5][:, 0:512], 5, 0, 512)
         quantize(4)
         multiply(4)
-
-        copy_by_fours(nc.vector.tensor_copy, 5, 0, VECTOR_PAIR_5)
-        for n0, n1 in HALVES:
-            add_and_activate(sums[LAST_RUN - 1][:, n0:n1], LAST_RUN - 1, n0, n1)
-        store(LAST_RUN - 1, 0, N)
+        copy_gpsimd(5, 0, 88)
+        copy_by_fours(nc.vector.tensor_copy, 5, 88, 152)
+        activate(5, 0, 512)
+        store(5, 0, 512)
+        copy_by_fours(nc.scalar.copy, 5, 152, 256)
+        add(sums[6][:, 0:512], 6, 0, 512)
+        activate(6, 0, 512)
+        store(6, 0, 512)
+        add(sums[7][:, 0:256], 7, 0, 256)
+        add(sums[7][:, 256:512], 7, 256, 512)
+        activate(7, 0, 256)
+        activate(7, 256, 512)
+        store(7, 0, 512)
         quantize(5)
         multiply(5)
-
-        for i in range(LAST_RUN, TILES):
-            for n0, n1 in HALVES:
-                add_and_activate(sums[i][:, n0:n1], i, n0, n1)
-                store(i, n0, n1)
+        add(sums[8][:, 0:256], 8, 0, 256)
+        add(sums[8][:, 256:512], 8, 256, 512)
+        activate(8, 0, 256)
+        store(8, 0, 256)
+        activate(8, 256, 512)
+        store(8, 256, 512)
+        add(sums[9][:, 0:256], 9, 0, 256)
+        add(sums[9][:, 256:512], 9, 256, 512)
+        activate(9, 0, 256)
+        store(9, 0, 256)
+        activate(9, 256, 512)
+        store(9, 256, 512)
+        add(sums[10][:, 0:256], 10, 0, 256)
+        add(sums[10][:, 256:512], 10, 256, 512)
+        activate(10, 0, 256)
+        store(10, 0, 256)
+        activate(10, 256, 512)
+        store(10, 256, 512)
+        add(sums[11][:, 0:256], 11, 0, 256)
+        add(sums[11][:, 256:512], 11, 256, 512)
+        activate(11, 0, 256)
+        store(11, 0, 256)
+        activate(11, 256, 512)
+        store(11, 256, 512)

@@ -25,7 +25,7 @@ HALF = N // 2
 HALVES = ((0, HALF), (HALF, N))
 CHUNKS = [PAIR] * PAIRS
 GATED = [3,4,5]
-OVERLAP = 8
+OVERLAP = 32
 SUM_BANKS = 7
 
 
@@ -45,7 +45,7 @@ def tile_mix_resid_tm_gelu_kernel(tc, x, w4_words, w4_scales, r8_words, r8_scale
         b_cols = keep.tile([P, 4], F32, name="b_cols")
         bias = keep.tile([P, N], F32, name="bias")
         ident = keep.tile([P, P], F32, name="ident")
-        staged = keep.tile([P, 4 * T], BF16, align_bytes=64, name="staged")
+        staged = keep.tile([P, 4 * T], BF16, align_bytes=256, name="staged")
         first_token = [r * PAIR - OVERLAP * len([g for g in GATED if g <= r]) for r in range(PAIRS)]
         grouped = [staged[:, 4 * t : 4 * (t + PAIR)] for t in first_token]
         codes = keep.tile([P, T], U32, align_bytes=64, name="codes")
@@ -149,15 +149,15 @@ def tile_mix_resid_tm_gelu_kernel(tc, x, w4_words, w4_scales, r8_words, r8_scale
             store(i, 0, N)
 
         first_sums = [psum.tile([P, N], F32, name="acc") for h in range(2)]
-        copy_by_fours(nc.vector.tensor_copy, 0, 0, 176)
-        copy_by_fours(nc.scalar.copy, 0, 176, 256)
+        copy_by_fours(nc.vector.tensor_copy, 0, 0, 192)
+        copy_by_fours(nc.scalar.copy, 0, 192, 256)
         spread_bias()
         quantize(0)
         for acc, (n0, n1) in zip(first_sums, HALVES):
             w4_pass(acc[:, :HALF], 0, n0, n1, start=True, stop=False)
         open_sum(1)
-        copy_by_fours(nc.vector.tensor_copy, 1, 0, 176)
-        copy_by_fours(nc.scalar.copy, 1, 176, 256)
+        copy_by_fours(nc.vector.tensor_copy, 1, 0, 192)
+        copy_by_fours(nc.scalar.copy, 1, 192, 256)
         quantize(1)
         for acc, (n0, n1) in zip(first_sums, HALVES):
             r8_pass(acc[:, :HALF], 0, n0, n1)
@@ -169,66 +169,82 @@ def tile_mix_resid_tm_gelu_kernel(tc, x, w4_words, w4_scales, r8_words, r8_scale
         activate(0, 0, 512)
         copy_by_fours(nc.vector.tensor_copy, 2, 0, 128)
         add(sums[1][:, 0:512], 1, 0, 512)
-        quantize(2)
-        multiply(2)
-        copy_gpsimd(3, 0, 80)
-        copy_by_fours(nc.vector.tensor_copy, 3, 80, 144)
-        copy_by_fours(nc.scalar.copy, 3, 144, 256)
+        quantize(2, P, PAIR)
+        quantize(2, 0, P)
+        open_sum(5)
+        close_sum(5)
+        open_sum(4)
+        close_sum(4)
+        copy_gpsimd(3, 0, 96)
+        copy_by_fours(nc.vector.tensor_copy, 3, 96, 128)
+        copy_by_fours(nc.scalar.copy, 3, 128, 256)
         activate(1, 0, 512)
         store_tiles(0, 2)
         add(sums[2][:, 0:512], 2, 0, 512)
         activate(2, 0, 512)
         store(2, 0, 512)
         add(sums[3][:, 0:512], 3, 0, 512)
-        quantize(3)
-        multiply(3)
-        copy_gpsimd(4, 0, 88)
-        copy_by_fours(nc.vector.tensor_copy, 4, 88, 152)
-        copy_by_fours(nc.scalar.copy, 4, 152, 256)
+        quantize(3, P, PAIR)
+        quantize(3, 0, P)
+        open_sum(7)
+        close_sum(7)
+        open_sum(6)
+        close_sum(6)
+        copy_gpsimd(4, 0, 128)
+        copy_by_fours(nc.vector.tensor_copy, 4, 128, 160)
+        copy_by_fours(nc.scalar.copy, 4, 160, 256)
         activate(3, 0, 512)
         store(3, 0, 512)
-        add(sums[4][:, 0:512], 4, 0, 512)
-        activate(4, 0, 512)
-        store(4, 0, 512)
         add(sums[5][:, 0:512], 5, 0, 512)
-        quantize(4)
-        multiply(4)
-        copy_gpsimd(5, 0, 88)
-        copy_by_fours(nc.vector.tensor_copy, 5, 88, 152)
         activate(5, 0, 512)
         store(5, 0, 512)
-        copy_by_fours(nc.scalar.copy, 5, 152, 256)
-        add(sums[6][:, 0:512], 6, 0, 512)
-        activate(6, 0, 512)
-        store(6, 0, 512)
-        add(sums[7][:, 0:256], 7, 0, 256)
-        add(sums[7][:, 256:512], 7, 256, 512)
-        activate(7, 0, 256)
-        activate(7, 256, 512)
+        add(sums[4][:, 0:512], 4, 0, 512)
+        quantize(4, P, PAIR)
+        quantize(4, 0, P)
+        open_sum(9)
+        close_sum(9)
+        open_sum(8)
+        close_sum(8)
+        copy_gpsimd(5, 0, 128)
+        copy_by_fours(nc.vector.tensor_copy, 5, 128, 160)
+        activate(4, 0, 512)
+        store(4, 0, 512)
+        copy_by_fours(nc.scalar.copy, 5, 160, 256)
+        add(sums[7][:, 0:512], 7, 0, 512)
+        activate(7, 0, 512)
         store(7, 0, 512)
-        quantize(5)
-        multiply(5)
-        add(sums[8][:, 0:256], 8, 0, 256)
-        add(sums[8][:, 256:512], 8, 256, 512)
-        activate(8, 0, 256)
-        store(8, 0, 256)
-        activate(8, 256, 512)
-        store(8, 256, 512)
+        add(sums[6][:, 0:256], 6, 0, 256)
+        add(sums[6][:, 256:512], 6, 256, 512)
+        activate(6, 0, 256)
+        activate(6, 256, 512)
+        store(6, 0, 512)
+        quantize(5, P, PAIR)
+        quantize(5, 0, P)
+        open_sum(11)
+        close_sum(11)
+        open_sum(10)
+        close_sum(10)
         add(sums[9][:, 0:256], 9, 0, 256)
         add(sums[9][:, 256:512], 9, 256, 512)
         activate(9, 0, 256)
         store(9, 0, 256)
         activate(9, 256, 512)
         store(9, 256, 512)
-        add(sums[10][:, 0:256], 10, 0, 256)
-        add(sums[10][:, 256:512], 10, 256, 512)
-        activate(10, 0, 256)
-        store(10, 0, 256)
-        activate(10, 256, 512)
-        store(10, 256, 512)
+        add(sums[8][:, 0:256], 8, 0, 256)
+        add(sums[8][:, 256:512], 8, 256, 512)
+        activate(8, 0, 256)
+        store(8, 0, 256)
+        activate(8, 256, 512)
+        store(8, 256, 512)
         add(sums[11][:, 0:256], 11, 0, 256)
         add(sums[11][:, 256:512], 11, 256, 512)
         activate(11, 0, 256)
         store(11, 0, 256)
         activate(11, 256, 512)
         store(11, 256, 512)
+        add(sums[10][:, 0:256], 10, 0, 256)
+        add(sums[10][:, 256:512], 10, 256, 512)
+        activate(10, 0, 256)
+        store(10, 0, 256)
+        activate(10, 256, 512)
+        store(10, 256, 512)

@@ -23,9 +23,15 @@ PAIR = 2 * P
 PAIRS = T // PAIR
 HALF = N // 2
 HALVES = ((0, HALF), (HALF, N))
-CHUNKS = [PAIR] * PAIRS
-GATED = [3,4,5]
-OVERLAP = 32
+CHUNKS = [P, 3 * P, PAIR, PAIR, PAIR, PAIR]
+STAGING = (0, 1, 1, 2, 2, 3)
+VECTOR_TILE_0 = 96
+VECTOR_PAIR_1 = 128
+GPSIMD_PAIR_2 = 96
+VECTOR_PAIR_3 = 144
+GPSIMD_PAIR_4 = 160
+VECTOR_PAIR_5 = 192
+LAST_RUN = 8
 SUM_BANKS = 7
 
 
@@ -45,9 +51,8 @@ def tile_mix_resid_tm_gelu_kernel(tc, x, w4_words, w4_scales, r8_words, r8_scale
         b_cols = keep.tile([P, 4], F32, name="b_cols")
         bias = keep.tile([P, N], F32, name="bias")
         ident = keep.tile([P, P], F32, name="ident")
-        staged = keep.tile([P, 4 * T], BF16, align_bytes=256, name="staged")
-        first_token = [r * PAIR - OVERLAP * len([g for g in GATED if g <= r]) for r in range(PAIRS)]
-        grouped = [staged[:, 4 * t : 4 * (t + PAIR)] for t in first_token]
+        stages = [keep.tile([P, 4 * PAIR], BF16, align_bytes=64, name=f"stage{r}") for r in range(max(STAGING) + 1)]
+        grouped = [stages[r] for r in STAGING]
         codes = keep.tile([P, T], U32, align_bytes=64, name="codes")
         x_plane = keep.tile([P, T], U8, align_bytes=64, name="x_plane")
         y = keep.tile([P, TILES * N], F32, name="y")
@@ -72,8 +77,8 @@ def tile_mix_resid_tm_gelu_kernel(tc, x, w4_words, w4_scales, r8_words, r8_scale
         make_identity(nc, ident[:], nomemset=True)
 
         load_x(0)
-        nc.sync.dma_start(out=b_cols[:], in_=b.rearrange("(p m) -> p m", m=4))
         nc.sync.dma_start(out=w4[:].bitcast(I32), in_=w4_words[0].bitcast(I32))
+        nc.sync.dma_start(out=b_cols[:], in_=b.rearrange("(p m) -> p m", m=4))
         load_scales(w4_plane, w4_scales)
         load_x(1)
         nc.sync.dma_start(out=r8[:].bitcast(I32), in_=r8_words[0].rearrange("p n i -> p (n i)").bitcast(I32))
@@ -129,122 +134,87 @@ def tile_mix_resid_tm_gelu_kernel(tc, x, w4_words, w4_scales, r8_words, r8_scale
                 open_sum(i)
                 close_sum(i)
 
-        def add(acc, i, n0, n1):
-            nc.vector.tensor_tensor(out=y[:, i * N + n0 : i * N + n1], in0=bias[:, n0:n1], in1=acc, op=ADD)
-
-        def activate(i, n0, n1):
+        def add_and_activate(acc, i, n0, n1):
             cols = slice(i * N + n0, i * N + n1)
+            nc.vector.tensor_tensor(out=y[:, cols], in0=bias[:, n0:n1], in1=acc, op=ADD)
             nc.scalar.activation(out=o[:, cols], in_=y[:, cols], func=GELU)
 
         def store(i, n0, n1):
             nc.sync.dma_start(out=out[i * P : (i + 1) * P, n0:n1], in_=o[:, i * N + n0 : i * N + n1])
 
-        def store_tiles(i, count):
-            nc.sync.dma_start(out=out[i * P : (i + count) * P, :].rearrange("(c p) n -> p c n", p=P),
-                              in_=o[:, i * N : (i + count) * N].rearrange("p (c n) -> p c n", n=N))
+        def add(i):
+            nc.vector.tensor_tensor(out=y[:, i * N : (i + 1) * N], in0=bias[:], in1=sums[i][:], op=ADD)
+
+        def activate_and_store(i):
+            nc.scalar.activation(out=o[:, i * N : (i + 1) * N], in_=y[:, i * N : (i + 1) * N], func=GELU)
+            store(i, 0, N)
 
         def finish(i):
-            add(sums[i][:], i, 0, N)
-            activate(i, 0, N)
+            add_and_activate(sums[i][:], i, 0, N)
             store(i, 0, N)
 
         first_sums = [psum.tile([P, N], F32, name="acc") for h in range(2)]
-        copy_by_fours(nc.vector.tensor_copy, 0, 0, 192)
-        copy_by_fours(nc.scalar.copy, 0, 192, 256)
+
+        copy_by_fours(nc.vector.tensor_copy, 0, 0, VECTOR_TILE_0)
+        copy_by_fours(nc.scalar.copy, 0, VECTOR_TILE_0, P)
         spread_bias()
-        quantize(0)
+        quantize(0, 0, P)
         for acc, (n0, n1) in zip(first_sums, HALVES):
-            w4_pass(acc[:, :HALF], 0, n0, n1, start=True, stop=False)
-        open_sum(1)
-        copy_by_fours(nc.vector.tensor_copy, 1, 0, 192)
-        copy_by_fours(nc.scalar.copy, 1, 192, 256)
-        quantize(1)
+            w4_pass(acc[:, :P], 0, n0, n0 + P, start=True, stop=False)
+            w4_pass(acc[:, P:HALF], 0, n0 + P, n1, start=False, stop=False)
+        unread = psum.tile([P, N], F32, name="acc")
+        for repeat in range(2):
+            w4_pass(unread[:], 0, 0, N, start=True, stop=True)
+        copy_by_fours(nc.vector.tensor_copy, 0, P, PAIR)
+        copy_by_fours(nc.scalar.copy, 1, VECTOR_PAIR_1, PAIR)
+        copy_by_fours(nc.vector.tensor_copy, 1, 0, VECTOR_PAIR_1)
+        quantize(0, P, PAIR)
         for acc, (n0, n1) in zip(first_sums, HALVES):
             r8_pass(acc[:, :HALF], 0, n0, n1)
+        open_sum(1)
         close_sum(1)
+        quantize(1)
         multiply(1)
-        add(first_sums[0][:, :HALF], 0, 0, HALF)
-        add(first_sums[1][:, :HALF], 0, HALF, N)
-        copy_by_fours(nc.scalar.copy, 2, 128, 256)
-        activate(0, 0, 512)
-        copy_by_fours(nc.vector.tensor_copy, 2, 0, 128)
-        add(sums[1][:, 0:512], 1, 0, 512)
-        quantize(2, P, PAIR)
-        quantize(2, 0, P)
-        open_sum(5)
-        close_sum(5)
-        open_sum(4)
-        close_sum(4)
-        copy_gpsimd(3, 0, 96)
-        copy_by_fours(nc.vector.tensor_copy, 3, 96, 128)
-        copy_by_fours(nc.scalar.copy, 3, 128, 256)
-        activate(1, 0, 512)
-        store_tiles(0, 2)
-        add(sums[2][:, 0:512], 2, 0, 512)
-        activate(2, 0, 512)
-        store(2, 0, 512)
-        add(sums[3][:, 0:512], 3, 0, 512)
-        quantize(3, P, PAIR)
-        quantize(3, 0, P)
-        open_sum(7)
-        close_sum(7)
-        open_sum(6)
-        close_sum(6)
-        copy_gpsimd(4, 0, 128)
-        copy_by_fours(nc.vector.tensor_copy, 4, 128, 160)
-        copy_by_fours(nc.scalar.copy, 4, 160, 256)
-        activate(3, 0, 512)
-        store(3, 0, 512)
-        add(sums[5][:, 0:512], 5, 0, 512)
-        activate(5, 0, 512)
-        store(5, 0, 512)
-        add(sums[4][:, 0:512], 4, 0, 512)
-        quantize(4, P, PAIR)
-        quantize(4, 0, P)
-        open_sum(9)
-        close_sum(9)
-        open_sum(8)
-        close_sum(8)
-        copy_gpsimd(5, 0, 128)
-        copy_by_fours(nc.vector.tensor_copy, 5, 128, 160)
-        activate(4, 0, 512)
-        store(4, 0, 512)
-        copy_by_fours(nc.scalar.copy, 5, 160, 256)
-        add(sums[7][:, 0:512], 7, 0, 512)
-        activate(7, 0, 512)
-        store(7, 0, 512)
-        add(sums[6][:, 0:256], 6, 0, 256)
-        add(sums[6][:, 256:512], 6, 256, 512)
-        activate(6, 0, 256)
-        activate(6, 256, 512)
-        store(6, 0, 512)
-        quantize(5, P, PAIR)
-        quantize(5, 0, P)
-        open_sum(11)
-        close_sum(11)
-        open_sum(10)
-        close_sum(10)
-        add(sums[9][:, 0:256], 9, 0, 256)
-        add(sums[9][:, 256:512], 9, 256, 512)
-        activate(9, 0, 256)
-        store(9, 0, 256)
-        activate(9, 256, 512)
-        store(9, 256, 512)
-        add(sums[8][:, 0:256], 8, 0, 256)
-        add(sums[8][:, 256:512], 8, 256, 512)
-        activate(8, 0, 256)
-        store(8, 0, 256)
-        activate(8, 256, 512)
-        store(8, 256, 512)
-        add(sums[11][:, 0:256], 11, 0, 256)
-        add(sums[11][:, 256:512], 11, 256, 512)
-        activate(11, 0, 256)
-        store(11, 0, 256)
-        activate(11, 256, 512)
-        store(11, 256, 512)
-        add(sums[10][:, 0:256], 10, 0, 256)
-        add(sums[10][:, 256:512], 10, 256, 512)
-        activate(10, 0, 256)
-        store(10, 0, 256)
-        activate(10, 256, 512)
-        store(10, 256, 512)
+
+        copy_gpsimd(2, 0, GPSIMD_PAIR_2)
+        (n0, n1), (n1, n2) = HALVES
+        add_and_activate(first_sums[0][:, :HALF], 0, n0, n1)
+        copy_by_fours(nc.scalar.copy, 2, GPSIMD_PAIR_2, PAIR)
+        add_and_activate(first_sums[1][:, :HALF], 0, n1, n2)
+        add_and_activate(sums[1][:], 1, 0, N)
+        nc.sync.dma_start(out=out[:PAIR, :].rearrange("(c p) n -> p c n", p=P), in_=o[:, : 2 * N].rearrange("p (c n) -> p c n", n=N))
+        add(2)
+        for lo in (0, P):
+            quantize(2, lo, lo + P)
+        multiply(2)
+
+        copy_by_fours(nc.vector.tensor_copy, 3, 0, VECTOR_PAIR_3)
+        copy_by_fours(nc.scalar.copy, 3, VECTOR_PAIR_3, PAIR)
+        activate_and_store(2)
+        finish(3)
+        for lo in (0, P):
+            quantize(3, lo, lo + P)
+        multiply(3)
+
+        copy_gpsimd(4, 0, GPSIMD_PAIR_4)
+        copy_by_fours(nc.scalar.copy, 4, GPSIMD_PAIR_4, PAIR)
+        finish(4)
+        copy_by_fours(nc.scalar.copy, 5, VECTOR_PAIR_5, PAIR)
+        for i in (5, 6):
+            finish(i)
+        for lo in (0, P):
+            quantize(4, lo, lo + P)
+        multiply(4)
+
+        copy_by_fours(nc.vector.tensor_copy, 5, 0, VECTOR_PAIR_5)
+        for n0, n1 in HALVES:
+            add_and_activate(sums[LAST_RUN - 1][:, n0:n1], LAST_RUN - 1, n0, n1)
+        store(LAST_RUN - 1, 0, N)
+        for lo in (0, P):
+            quantize(5, lo, lo + P)
+        multiply(5)
+
+        for i in range(LAST_RUN, TILES):
+            for n0, n1 in HALVES:
+                add_and_activate(sums[i][:, n0:n1], i, n0, n1)
+                store(i, n0, n1)

@@ -20,17 +20,15 @@ ADD = mybir.AluOpType.add
 P = 128
 TILES = T // P
 PAIR = 2 * P
-PAIRS = T // PAIR
 HALF = N // 2
 HALVES = ((0, HALF), (HALF, N))
-CHUNKS = [P, 3 * P, PAIR, PAIR, PAIR, PAIR]
-STAGING = (0, 1, 1, 2, 2, 3)
+CHUNKS = [P, 3 * P, P, PAIR, PAIR, 3 * P]
+STAGING = ((0, 0), (0, 1), (1, 0), (1, 1), (2, 0), (2, 0), (2, 1), (3, 0), (3, 1), (3, 0), (3, 1), (3, 2))
+STAGE_SLOTS = (2, 2, 2, 3)
 VECTOR_TILE_0 = 96
-VECTOR_PAIR_1 = 128
-GPSIMD_PAIR_2 = 96
-VECTOR_PAIR_3 = 144
-GPSIMD_PAIR_4 = 160
-VECTOR_PAIR_5 = 192
+VECTOR_TILE_4 = 64
+VECTOR_TILES_7_8 = 160
+GPSIMD_TILES_9_10 = 160
 LAST_RUN = 8
 SUM_BANKS = 7
 
@@ -51,8 +49,7 @@ def tile_mix_resid_tm_gelu_kernel(tc, x, w4_words, w4_scales, r8_words, r8_scale
         b_cols = keep.tile([P, 4], F32, name="b_cols")
         bias = keep.tile([P, N], F32, name="bias")
         ident = keep.tile([P, P], F32, name="ident")
-        stages = [keep.tile([P, 4 * PAIR], BF16, align_bytes=64, name=f"stage{r}") for r in range(max(STAGING) + 1)]
-        grouped = [stages[r] for r in STAGING]
+        stages = [keep.tile([P, 4 * w * P], BF16, align_bytes=64, name=f"stage{r}") for r, w in enumerate(STAGE_SLOTS)]
         codes = keep.tile([P, T], U32, align_bytes=64, name="codes")
         x_plane = keep.tile([P, T], U8, align_bytes=64, name="x_plane")
         y = keep.tile([P, TILES * N], F32, name="y")
@@ -77,8 +74,8 @@ def tile_mix_resid_tm_gelu_kernel(tc, x, w4_words, w4_scales, r8_words, r8_scale
         make_identity(nc, ident[:], nomemset=True)
 
         load_x(0)
-        nc.sync.dma_start(out=w4[:].bitcast(I32), in_=w4_words[0].bitcast(I32))
         nc.sync.dma_start(out=b_cols[:], in_=b.rearrange("(p m) -> p m", m=4))
+        nc.sync.dma_start(out=w4[:].bitcast(I32), in_=w4_words[0].bitcast(I32))
         load_scales(w4_plane, w4_scales)
         load_x(1)
         nc.sync.dma_start(out=r8[:].bitcast(I32), in_=r8_words[0].rearrange("p n i -> p (n i)").bitcast(I32))
@@ -94,23 +91,24 @@ def tile_mix_resid_tm_gelu_kernel(tc, x, w4_words, w4_scales, r8_words, r8_scale
                 nc.tensor.transpose(b_ps[:, m, :], b_cols[:, m : m + 1].to_broadcast([P, P]), ident[:])
             nc.scalar.copy(out=bias[:].rearrange("t (p m) -> t p m", m=4), in_=b_ps[:].rearrange("t m p -> t p m"))
 
-        def sides(pair, lo, hi):
-            t0 = pair * PAIR + lo
+        def sides(i, lo, hi):
+            t0 = i * P + lo
             c = max(j for j in range(len(CHUNKS)) if starts[j] <= t0)
-            return raws[c][:, :, t0 - starts[c] : t0 - starts[c] + hi - lo], grouped[pair][:, 4 * lo : 4 * hi]
+            r, slot = STAGING[i]
+            return raws[c][:, :, t0 - starts[c] : t0 - starts[c] + hi - lo], stages[r][:, 4 * (slot * P + lo) : 4 * (slot * P + hi)]
 
-        def copy_by_fours(copy, pair, lo, hi):
-            src, dst = sides(pair, lo, hi)
+        def copy_by_fours(copy, i, lo, hi):
+            src, dst = sides(i, lo, hi)
             copy(out=dst.rearrange("p (c i j) -> p c j i", i=4, j=4), in_=src.rearrange("p j (c i) -> p c j i", i=4))
 
-        def copy_gpsimd(pair, lo, hi):
-            src, dst = sides(pair, lo, hi)
+        def copy_gpsimd(i, lo, hi):
+            src, dst = sides(i, lo, hi)
             nc.gpsimd.tensor_scalar(out=dst.rearrange("p (w j) -> p w j", j=4), in0=src.rearrange("p j w -> p w j"),
                                     scalar1=1.0, scalar2=0.0, op0=MULT, op1=ADD)
 
-        def quantize(pair, lo=0, hi=PAIR):
-            cols = slice(pair * PAIR + lo, pair * PAIR + hi)
-            nc.vector.quantize_mx(out=codes[:, cols].bitcast(FP8X4), scales=x_plane[:, cols], in_=grouped[pair][:, 4 * lo : 4 * hi])
+        def quantize(i, tiles=1):
+            cols = slice(i * P, (i + tiles) * P)
+            nc.vector.quantize_mx(out=codes[:, cols].bitcast(FP8X4), scales=x_plane[:, cols], in_=sides(i, 0, tiles * P)[1])
 
         def w4_pass(acc, i, n0, n1, start, stop):
             cols = slice(i * P, (i + 1) * P)
@@ -129,10 +127,15 @@ def tile_mix_resid_tm_gelu_kernel(tc, x, w4_words, w4_scales, r8_words, r8_scale
         def close_sum(i):
             r8_pass(sums[i][:], i, 0, N)
 
-        def multiply(pair):
-            for i in (2 * pair, 2 * pair + 1):
-                open_sum(i)
-                close_sum(i)
+        def multiply(i):
+            open_sum(i)
+            close_sum(i)
+
+        def quantize_and_multiply(tiles):
+            for i in tiles:
+                quantize(i)
+            for i in tiles:
+                multiply(i)
 
         def add_and_activate(acc, i, n0, n1):
             cols = slice(i * N + n0, i * N + n1)
@@ -158,63 +161,57 @@ def tile_mix_resid_tm_gelu_kernel(tc, x, w4_words, w4_scales, r8_words, r8_scale
         copy_by_fours(nc.vector.tensor_copy, 0, 0, VECTOR_TILE_0)
         copy_by_fours(nc.scalar.copy, 0, VECTOR_TILE_0, P)
         spread_bias()
-        quantize(0, 0, P)
+        quantize(0)
         for acc, (n0, n1) in zip(first_sums, HALVES):
             w4_pass(acc[:, :P], 0, n0, n0 + P, start=True, stop=False)
             w4_pass(acc[:, P:HALF], 0, n0 + P, n1, start=False, stop=False)
         unread = psum.tile([P, N], F32, name="acc")
         for repeat in range(2):
             w4_pass(unread[:], 0, 0, N, start=True, stop=True)
-        copy_by_fours(nc.vector.tensor_copy, 0, P, PAIR)
-        copy_by_fours(nc.scalar.copy, 1, VECTOR_PAIR_1, PAIR)
-        copy_by_fours(nc.vector.tensor_copy, 1, 0, VECTOR_PAIR_1)
-        quantize(0, P, PAIR)
+        copy_by_fours(nc.vector.tensor_copy, 1, 0, P)
+        copy_by_fours(nc.scalar.copy, 3, 0, P)
+        copy_by_fours(nc.vector.tensor_copy, 2, 0, P)
+        quantize(1)
         for acc, (n0, n1) in zip(first_sums, HALVES):
             r8_pass(acc[:, :HALF], 0, n0, n1)
-        open_sum(1)
-        close_sum(1)
-        quantize(1)
         multiply(1)
-
-        copy_gpsimd(2, 0, GPSIMD_PAIR_2)
-        (n0, n1), (n1, n2) = HALVES
-        add_and_activate(first_sums[0][:, :HALF], 0, n0, n1)
-        copy_by_fours(nc.scalar.copy, 2, GPSIMD_PAIR_2, PAIR)
-        add_and_activate(first_sums[1][:, :HALF], 0, n1, n2)
-        add_and_activate(sums[1][:], 1, 0, N)
-        nc.sync.dma_start(out=out[:PAIR, :].rearrange("(c p) n -> p c n", p=P), in_=o[:, : 2 * N].rearrange("p (c n) -> p c n", n=N))
-        add(2)
-        for lo in (0, P):
-            quantize(2, lo, lo + P)
+        quantize(2, 2)
         multiply(2)
-
-        copy_by_fours(nc.vector.tensor_copy, 3, 0, VECTOR_PAIR_3)
-        copy_by_fours(nc.scalar.copy, 3, VECTOR_PAIR_3, PAIR)
-        activate_and_store(2)
-        finish(3)
-        for lo in (0, P):
-            quantize(3, lo, lo + P)
         multiply(3)
 
-        copy_gpsimd(4, 0, GPSIMD_PAIR_4)
-        copy_by_fours(nc.scalar.copy, 4, GPSIMD_PAIR_4, PAIR)
-        finish(4)
-        copy_by_fours(nc.scalar.copy, 5, VECTOR_PAIR_5, PAIR)
-        for i in (5, 6):
-            finish(i)
-        for lo in (0, P):
-            quantize(4, lo, lo + P)
-        multiply(4)
+        copy_by_fours(nc.scalar.copy, 4, VECTOR_TILE_4, P)
+        (n0, n1), (n1, n2) = HALVES
+        add_and_activate(first_sums[0][:, :HALF], 0, n0, n1)
+        copy_by_fours(nc.vector.tensor_copy, 4, 0, VECTOR_TILE_4)
+        add_and_activate(first_sums[1][:, :HALF], 0, n1, n2)
+        quantize_and_multiply((4,))
+        add(1)
 
-        copy_by_fours(nc.vector.tensor_copy, 5, 0, VECTOR_PAIR_5)
-        for n0, n1 in HALVES:
-            add_and_activate(sums[LAST_RUN - 1][:, n0:n1], LAST_RUN - 1, n0, n1)
-        store(LAST_RUN - 1, 0, N)
-        for lo in (0, P):
-            quantize(5, lo, lo + P)
-        multiply(5)
+        copy_gpsimd(5, 0, P)
+        copy_by_fours(nc.scalar.copy, 6, 0, P)
+        nc.scalar.activation(out=o[:, N : 2 * N], in_=y[:, N : 2 * N], func=GELU)
+        nc.sync.dma_start(out=out[:PAIR, :].rearrange("(c p) n -> p c n", p=P), in_=o[:, : 2 * N].rearrange("p (c n) -> p c n", n=N))
+        finish(2)
+        add(3)
+        quantize_and_multiply((6, 5))
+        copy_by_fours(nc.scalar.copy, 7, VECTOR_TILES_7_8, PAIR)
+        activate_and_store(3)
+        copy_by_fours(nc.vector.tensor_copy, 7, 0, VECTOR_TILES_7_8)
+        add(4)
+        quantize_and_multiply((7, 8))
+        activate_and_store(4)
 
+        copy_gpsimd(9, 0, GPSIMD_TILES_9_10)
+        copy_by_fours(nc.scalar.copy, 9, GPSIMD_TILES_9_10, PAIR)
+        finish(6)
+        finish(5)
+        add(7)
+        quantize_and_multiply((9, 10))
+        copy_by_fours(nc.vector.tensor_copy, 11, 0, P)
+        activate_and_store(7)
         for i in range(LAST_RUN, TILES):
             for n0, n1 in HALVES:
                 add_and_activate(sums[i][:, n0:n1], i, n0, n1)
                 store(i, n0, n1)
+            if i == LAST_RUN:
+                quantize_and_multiply((11,))

@@ -27,8 +27,9 @@ STAGING = ((0, 0), (0, 1), (1, 0), (1, 1), (2, 0), (2, 0), (2, 1), (3, 0), (3, 1
 STAGE_SLOTS = (2, 2, 2, 3)
 VECTOR_TILE_0 = 96
 VECTOR_TILE_4 = 64
+GPSIMD_TILE_5 = 96
 VECTOR_TILES_7_8 = 160
-GPSIMD_TILES_9_10 = 160
+GPSIMD_TILES_9_10 = 128
 LAST_RUN = 8
 SUM_BANKS = 7
 
@@ -187,8 +188,8 @@ def tile_mix_resid_tm_gelu_kernel(tc, x, w4_words, w4_scales, r8_words, r8_scale
         quantize_and_multiply((4,))
         add(1)
 
-        copy_gpsimd(5, 0, P)
-        copy_by_fours(nc.scalar.copy, 6, 0, P)
+        copy_gpsimd(5, 0, GPSIMD_TILE_5)
+        copy_by_fours(nc.scalar.copy, 5, GPSIMD_TILE_5, PAIR)
         nc.scalar.activation(out=o[:, N : 2 * N], in_=y[:, N : 2 * N], func=GELU)
         nc.sync.dma_start(out=out[:PAIR, :].rearrange("(c p) n -> p c n", p=P), in_=o[:, : 2 * N].rearrange("p (c n) -> p c n", n=N))
         finish(2)

@@ -27,9 +27,9 @@ STAGING = ((0, 0), (0, 1), (1, 0), (1, 1), (2, 0), (2, 0), (2, 1), (3, 0), (3, 1
 STAGE_SLOTS = (2, 2, 2, 3)
 VECTOR_TILE_0 = 96
 VECTOR_TILE_4 = 64
-GPSIMD_TILE_5 = 96
+GPSIMD_TILE_5 = 112
 VECTOR_TILES_7_8 = 160
-GPSIMD_TILES_9_10 = 128
+GPSIMD_TILES_9_10 = 144
 LAST_RUN = 8
 SUM_BANKS = 7
 
@@ -67,12 +67,12 @@ def tile_mix_resid_tm_gelu_kernel(tc, x, w4_words, w4_scales, r8_words, r8_scale
             for r in range(4):
                 nc.sync.dma_start(out=plane[r:P:32, :].bitcast(I32), in_=scales[0, r:16:4, :].bitcast(I32))
 
-        nc.gpsimd.memset(w4_plane[:].bitcast(I32), 0)
-        nc.vector.memset(r8_plane[:].bitcast(I32), 0)
-        nc.vector.memset(ident[:], 0.0)
+        nc.vector.memset(w4_plane[:].bitcast(I32), 0)
         nc.vector.memset(warm[:], 0.0)
         nc.scalar.activation(out=warm[:], in_=warm[:], func=GELU)
+        nc.vector.memset(ident[:], 0.0)
         make_identity(nc, ident[:], nomemset=True)
+        nc.vector.memset(r8_plane[:].bitcast(I32), 0)
 
         load_x(0)
         nc.sync.dma_start(out=b_cols[:], in_=b.rearrange("(p m) -> p m", m=4))

from contextlib import ExitStack

import concourse.mybir as mybir
from concourse.masks import make_identity

K, N, T = 512, 512, 1536
FLOPS = 2 * 2 * K * N * T

F32 = mybir.dt.float32
BF16 = mybir.dt.bfloat16
I32 = mybir.dt.int32
U32 = mybir.dt.uint32
U8 = mybir.dt.uint8
FP8X4 = mybir.dt.float8_e4m3fn_x4
FP4X4 = mybir.dt.float4_e2m1fn_x4
GELU = mybir.ActivationFunctionType.Gelu_apprx_tanh
MULT = mybir.AluOpType.mult
ADD = mybir.AluOpType.add

P = 128
TILES = T // P
PAIR = 2 * P
HALF = N // 2
HALVES = ((0, HALF), (HALF, N))
CHUNKS = [P, 3 * P, P, PAIR, PAIR, 3 * P]
STAGING = ((0, 0), (0, 1), (1, 0), (1, 1), (2, 0), (2, 0), (2, 1), (3, 0), (3, 1), (3, 0), (3, 1), (3, 2))
STAGE_SLOTS = (2, 2, 2, 3)
VECTOR_TILE_0 = 96
VECTOR_TILE_4 = 64
GPSIMD_TILE_5 = 112
VECTOR_TILES_7_8 = 160
GPSIMD_TILES_9_10 = 144
LAST_RUN = 8
SUM_BANKS = 7


def tile_mix_resid_tm_gelu_kernel(tc, x, w4_words, w4_scales, r8_words, r8_scales, b, out):
    nc = tc.nc
    with ExitStack() as ctx:
        keep = ctx.enter_context(tc.tile_pool(name="keep", bufs=1))
        psum = ctx.enter_context(tc.psum_pool(name="psum", bufs=SUM_BANKS))
        psum_b = ctx.enter_context(tc.psum_pool(name="psum_b", bufs=1))
        ctx.enter_context(tc.manual_schedule())

        w4_plane = keep.tile([P, N], U8, align_bytes=64, name="w4_plane")
        r8_plane = keep.tile([P, N], U8, align_bytes=64, name="r8_plane")
        w4 = keep.tile([P, 2 * N], U8, align_bytes=64, name="w4")
        r8 = keep.tile([P, 4 * N], U8, align_bytes=64, name="r8")
        warm = keep.tile([P, 1], F32, name="warm")
        b_cols = keep.tile([P, 4], F32, name="b_cols")
        bias = keep.tile([P, N], F32, name="bias")
        ident = keep.tile([P, P], F32, name="ident")
        stages = [keep.tile([P, 4 * w * P], BF16, align_bytes=64, name=f"stage{r}") for r, w in enumerate(STAGE_SLOTS)]
        codes = keep.tile([P, T], U32, align_bytes=64, name="codes")
        x_plane = keep.tile([P, T], U8, align_bytes=64, name="x_plane")
        y = keep.tile([P, TILES * N], F32, name="y")
        o = keep.tile([P, TILES * N], F32, name="o")

        xv = x.rearrange("(p j) t -> p j t", j=4)
        starts = [sum(CHUNKS[:c]) for c in range(len(CHUNKS))]
        raws = [keep.tile([P, 4, w], F32, name=f"raw{c}") for c, w in enumerate(CHUNKS)]

        def load_x(c):
            nc.sync.dma_start(out=raws[c][:], in_=xv[:, :, starts[c] : starts[c] + CHUNKS[c]])

        def load_scales(plane, scales):
            for r in range(4):
                nc.sync.dma_start(out=plane[r:P:32, :].bitcast(I32), in_=scales[0, r:16:4, :].bitcast(I32))

        nc.vector.memset(w4_plane[:].bitcast(I32), 0)
        nc.vector.memset(warm[:], 0.0)
        nc.scalar.activation(out=warm[:], in_=warm[:], func=GELU)
        nc.vector.memset(ident[:], 0.0)
        make_identity(nc, ident[:], nomemset=True)
        nc.vector.memset(r8_plane[:].bitcast(I32), 0)

        load_x(0)
        nc.sync.dma_start(out=b_cols[:], in_=b.rearrange("(p m) -> p m", m=4))
        nc.sync.dma_start(out=w4[:].bitcast(I32), in_=w4_words[0].bitcast(I32))
        load_scales(w4_plane, w4_scales)
        load_x(1)
        nc.sync.dma_start(out=r8[:].bitcast(I32), in_=r8_words[0].rearrange("p n i -> p (n i)").bitcast(I32))
        load_scales(r8_plane, r8_scales)
        for c in range(2, len(CHUNKS)):
            load_x(c)

        b_ps = psum_b.tile([P, 4, P], F32, name="b_ps")
        sums = {}

        def spread_bias():
            for m in range(4):
                nc.tensor.transpose(b_ps[:, m, :], b_cols[:, m : m + 1].to_broadcast([P, P]), ident[:])
            nc.scalar.copy(out=bias[:].rearrange("t (p m) -> t p m", m=4), in_=b_ps[:].rearrange("t m p -> t p m"))

        def sides(i, lo, hi):
            t0 = i * P + lo
            c = max(j for j in range(len(CHUNKS)) if starts[j] <= t0)
            r, slot = STAGING[i]
            return raws[c][:, :, t0 - starts[c] : t0 - starts[c] + hi - lo], stages[r][:, 4 * (slot * P + lo) : 4 * (slot * P + hi)]

        def copy_by_fours(copy, i, lo, hi):
            src, dst = sides(i, lo, hi)
            copy(out=dst.rearrange("p (c i j) -> p c j i", i=4, j=4), in_=src.rearrange("p j (c i) -> p c j i", i=4))

        def copy_gpsimd(i, lo, hi):
            src, dst = sides(i, lo, hi)
            nc.gpsimd.tensor_scalar(out=dst.rearrange("p (w j) -> p w j", j=4), in0=src.rearrange("p j w -> p w j"),
                                    scalar1=1.0, scalar2=0.0, op0=MULT, op1=ADD)

        def quantize(i, tiles=1):
            cols = slice(i * P, (i + tiles) * P)
            nc.vector.quantize_mx(out=codes[:, cols].bitcast(FP8X4), scales=x_plane[:, cols], in_=sides(i, 0, tiles * P)[1])

        def w4_pass(acc, i, n0, n1, start, stop):
            cols = slice(i * P, (i + 1) * P)
            nc.tensor.matmul_mx(out=acc, lhsT=codes[:, cols].bitcast(FP8X4), lhsT_scale=x_plane[:, cols],
                                rhs=w4[:, 2 * n0 : 2 * n1].bitcast(FP4X4), rhs_scale=w4_plane[:, n0:n1], start=start, stop=stop)

        def r8_pass(acc, i, n0, n1):
            cols = slice(i * P, (i + 1) * P)
            nc.tensor.matmul_mx(out=acc, lhsT=codes[:, cols].bitcast(FP8X4), lhsT_scale=x_plane[:, cols],
                                rhs=r8[:, 4 * n0 : 4 * n1].bitcast(FP8X4), rhs_scale=r8_plane[:, n0:n1], start=False, stop=True)

        def open_sum(i):
            sums[i] = psum.tile([P, N], F32, name="acc")
            w4_pass(sums[i][:], i, 0, N, start=True, stop=False)

        def close_sum(i):
            r8_pass(sums[i][:], i, 0, N)

        def multiply(i):
            open_sum(i)
            close_sum(i)

        def quantize_and_multiply(tiles):
            for i in tiles:
                quantize(i)
            for i in tiles:
                multiply(i)

        def add_and_activate(acc, i, n0, n1):
            cols = slice(i * N + n0, i * N + n1)
            nc.vector.tensor_tensor(out=y[:, cols], in0=bias[:, n0:n1], in1=acc, op=ADD)
            nc.scalar.activation(out=o[:, cols], in_=y[:, cols], func=GELU)

        def store(i, n0, n1):
            nc.sync.dma_start(out=out[i * P : (i + 1) * P, n0:n1], in_=o[:, i * N + n0 : i * N + n1])

        def add(i):
            nc.vector.tensor_tensor(out=y[:, i * N : (i + 1) * N], in0=bias[:], in1=sums[i][:], op=ADD)

        def activate_and_store(i):
            nc.scalar.activation(out=o[:, i * N : (i + 1) * N], in_=y[:, i * N : (i + 1) * N], func=GELU)
            store(i, 0, N)

        def finish(i):
            add_and_activate(sums[i][:], i, 0, N)
            store(i, 0, N)

        first_sums = [psum.tile([P, N], F32, name="acc") for h in range(2)]

        copy_by_fours(nc.vector.tensor_copy, 0, 0, VECTOR_TILE_0)
        copy_by_fours(nc.scalar.copy, 0, VECTOR_TILE_0, P)
        spread_bias()
        quantize(0)
        for acc, (n0, n1) in zip(first_sums, HALVES):
            w4_pass(acc[:, :P], 0, n0, n0 + P, start=True, stop=False)
            w4_pass(acc[:, P:HALF], 0, n0 + P, n1, start=False, stop=False)
        unread = psum.tile([P, N], F32, name="acc")
        for repeat in range(2):
            w4_pass(unread[:], 0, 0, N, start=True, stop=True)
        copy_by_fours(nc.vector.tensor_copy, 1, 0, P)
        copy_by_fours(nc.scalar.copy, 3, 0, P)
        copy_by_fours(nc.vector.tensor_copy, 2, 0, P)
        quantize(1)
        for acc, (n0, n1) in zip(first_sums, HALVES):
            r8_pass(acc[:, :HALF], 0, n0, n1)
        multiply(1)
        quantize(2, 2)
        multiply(2)
        multiply(3)

        copy_by_fours(nc.scalar.copy, 4, VECTOR_TILE_4, P)
        (n0, n1), (n1, n2) = HALVES
        add_and_activate(first_sums[0][:, :HALF], 0, n0, n1)
        copy_by_fours(nc.vector.tensor_copy, 4, 0, VECTOR_TILE_4)
        add_and_activate(first_sums[1][:, :HALF], 0, n1, n2)
        quantize_and_multiply((4,))
        add(1)

        copy_gpsimd(5, 0, GPSIMD_TILE_5)
        copy_by_fours(nc.scalar.copy, 5, GPSIMD_TILE_5, PAIR)
        nc.scalar.activation(out=o[:, N : 2 * N], in_=y[:, N : 2 * N], func=GELU)
        nc.sync.dma_start(out=out[:PAIR, :].rearrange("(c p) n -> p c n", p=P), in_=o[:, : 2 * N].rearrange("p (c n) -> p c n", n=N))
        finish(2)
        add(3)
        quantize_and_multiply((6, 5))
        copy_by_fours(nc.scalar.copy, 7, VECTOR_TILES_7_8, PAIR)
        activate_and_store(3)
        copy_by_fours(nc.vector.tensor_copy, 7, 0, VECTOR_TILES_7_8)
        add(4)
        quantize_and_multiply((7, 8))
        activate_and_store(4)

        copy_gpsimd(9, 0, GPSIMD_TILES_9_10)
        copy_by_fours(nc.scalar.copy, 9, GPSIMD_TILES_9_10, PAIR)
        finish(6)
        finish(5)
        add(7)
        quantize_and_multiply((9, 10))
        copy_by_fours(nc.vector.tensor_copy, 11, 0, P)
        activate_and_store(7)
        for i in range(LAST_RUN, TILES):
            for n0, n1 in HALVES:
                add_and_activate(sums[i][:, n0:n1], i, n0, n1)
                store(i, n0, n1)
            if i == LAST_RUN:
                quantize_and_multiply((11,))
